import numpy as np
import ml_dtypes


def mxq(x, axis, fmt="e4m3"):
    dtype, down = {"e4m3": (ml_dtypes.float8_e4m3fn, 7), "e5m2": (ml_dtypes.float8_e5m2, 14)}[fmt]
    v = np.moveaxis(np.asarray(x, np.float32).astype(ml_dtypes.bfloat16).astype(np.float64), axis, -1)
    blocks = v.reshape(v.shape[:-1] + (-1, 32))
    amax = np.abs(blocks).max(-1, keepdims=True)
    byte = np.maximum(np.where(amax > 0, np.frexp(amax)[1] - 1 + 127, 0) - down, 1)
    scale = np.exp2(byte - 127.0)
    codes = (blocks / scale).astype(np.float32).astype(dtype).astype(np.float64)
    return np.moveaxis((codes * scale).reshape(v.shape), -1, axis)


WIDE = False


def mx_kscale(k):
    if not WIDE:
        return np.ones(k)
    levels = np.array([24, -24, 12, -12, 0])
    if k % 512:
        return np.exp2(np.random.permutation(np.resize(levels, k // 32))).repeat(32)
    a = np.empty((k // 512, 16))
    for p in range(k // 512):
        a[p, :8] = np.random.permutation(np.resize(levels, 8))
        for g in range(8):
            far = levels[np.abs(levels - a[p, g]) >= 10]
            a[p, g + 8] = far[np.random.randint(len(far))]
    return np.exp2(a.ravel()).repeat(32)


def f64(x):
    return np.asarray(x).astype(np.float64)


def striped(idx):
    return np.tile(idx.reshape(-1, 16).T, (8, 1)).astype(np.uint16)


def unstriped(offs):
    return offs[:16].T.reshape(-1).astype(np.int64)


E2M1 = np.array([0.0, 0.5, 1.0, 1.5, 2.0, 3.0, 4.0, 6.0, -0.0, -0.5, -1.0, -1.5, -2.0, -3.0, -4.0, -6.0])


def pack_weight(w, fmt):
    k, n = w.shape
    w = f64(np.asarray(w, np.float32).astype(ml_dtypes.bfloat16)).reshape(k // 32, 32, n)
    amax = np.abs(w).max(1)
    if fmt == "e4m3":
        byte = np.frexp(amax)[1] - 1 + 127 - 7
    else:
        mant, ex = np.frexp(amax / 6.0)
        byte = np.where(mant > 0.5, ex, ex - 1) + 127
    byte = np.clip(np.where(amax > 0, byte, 1), 1, 254)
    scaled = (w * np.exp2(127.0 - byte)[:, None, :]).reshape(k, n).astype(np.float32)
    by_word = np.ascontiguousarray(scaled.reshape(k // 512, 128, 4, n).transpose(0, 1, 3, 2))
    if fmt == "e4m3":
        words = by_word.astype(ml_dtypes.float8_e4m3fn).view(np.uint8)
    else:
        c = by_word.astype(ml_dtypes.float4_e2m1fn).view(np.uint8) & 0xF
        words = (c[..., 0::2] | (c[..., 1::2] << 4)).reshape(k // 512, 128, 2 * n)
    return np.ascontiguousarray(words), np.ascontiguousarray(byte.astype(np.uint8).reshape(k // 512, 16, n))


def unpack_weight(words, scales, fmt):
    g, _, n = scales.shape
    words = np.ascontiguousarray(words).reshape(g, 128, n, -1)
    if fmt == "e4m3":
        vals = words.view(ml_dtypes.float8_e4m3fn).astype(np.float64)
    else:
        nib = np.empty((g, 128, n, 4), np.uint8)
        nib[..., 0::2] = words & 0xF
        nib[..., 1::2] = words >> 4
        vals = E2M1[nib]
    vals = vals * np.repeat(np.exp2(scales.astype(np.float64) - 127.0), 8, axis=1)[..., None]
    return vals.transpose(0, 1, 3, 2).reshape(g * 512, n)


def planes(y):
    n, m = y.shape
    v = y.astype(np.float32).astype(ml_dtypes.bfloat16).astype(np.float64).reshape(n // 32, 32, m)
    top = np.abs(v).max(1)
    byte = np.clip(np.where(top > 0, np.frexp(top)[1] - 1 + 127 - 7, 1), 1, 254)
    codes = (v * np.exp2(127.0 - byte)[:, None, :]).reshape(n, m).astype(np.float32).astype(ml_dtypes.float8_e4m3fn).view(np.uint8)
    words = codes.reshape(n // 512, 128, 4, m).transpose(0, 1, 3, 2)
    return np.ascontiguousarray(words), np.ascontiguousarray(byte.astype(np.uint8).reshape(n // 512, 16, m))


def sigm(f):
    return 1.0 / (1.0 + np.exp(-np.maximum(f, -700.0)))


K, N, T, J = 512, 512, 2048, 1024


def setup_inputs():
    n = np.random.standard_normal
    s = mx_kscale(K)[:, None]
    p_tab = pack_weight(n((K, T)) * s, "e4m3")
    p_wa = pack_weight(n((K, N)) / np.sqrt(2 * K) / s, "e4m3")
    p_wc = pack_weight(n((K, N)) / np.sqrt(K) / s, "e4m3")
    return {
        "tab_words": p_tab[0],
        "tab_scales": p_tab[1],
        "wa_words": p_wa[0],
        "wa_scales": p_wa[1],
        "wb": (n((K, N)) / np.sqrt(2 * K) / s).astype(np.float32),
        "wc_words": p_wc[0],
        "wc_scales": p_wc[1],
        "rT": (n((N, T))).astype(np.float32),
        "wgo": np.tile(np.random.uniform(0.5, 2.0, J), (128, 1)).astype(np.float32),
        "offs": striped(np.random.permutation(T)[:J]),
        "offs2": striped(np.random.permutation(T)[:J]),
    }


def reference(tab_words, tab_scales, wa_words, wa_scales, wb, wc_words, wc_scales, rT, wgo, offs, offs2):
    idx = unstriped(offs)
    idx2 = unstriped(offs2)
    tab_ = unpack_weight(tab_words, tab_scales, "e4m3")[:, idx]
    tabb_ = unpack_weight(tab_words, tab_scales, "e4m3")[:, idx2]
    wa_ = unpack_weight(wa_words, wa_scales, "e4m3")
    wb_ = mxq(f64(wb), 0, "e4m3")
    za = wa_.T @ tabb_ + wb_.T @ tab_
    eta = sigm(za)
    wc_ = unpack_weight(wc_words, wc_scales, "e4m3")
    ms = wc_.T @ tab_
    out = np.zeros((N, T))
    out[:, idx2] = f64(wgo)[0] * (eta * ms + f64(rT)[:, idx2])
    return (out,) + planes(out)

@@ -1,0 +1,205 @@
+from contextlib import ExitStack
+
+import concourse.mybir as mybir
+from concourse.masks import make_identity
+
+K, N, T, J = 512, 512, 2048, 1024
+FLOPS = 3 * 2 * K * N * J
+
+F32 = mybir.dt.float32
+BF16 = mybir.dt.bfloat16
+I32 = mybir.dt.int32
+U32 = mybir.dt.uint32
+U16 = mybir.dt.uint16
+U8 = mybir.dt.uint8
+FP8X4 = mybir.dt.float8_e4m3fn_x4
+MULT = mybir.AluOpType.mult
+SIGMOID = mybir.ActivationFunctionType.Sigmoid
+
+P = 128
+PACK = 4
+HALF = J // 2
+CHUNKS = J // P
+BANK = 512
+PER_BANK = BANK // P
+QCOLS = 512
+PIECES = T // QCOLS
+VECTOR_PIECES = 2
+SRC, TGT = 0, 1
+
+
+def tile_list_rgg_LP_kernel(
+    tc, tab_words, tab_scales, wa_words, wa_scales, wb, wc_words, wc_scales, rT, wgo, offs, offs2, out_0, out_1, out_2
+):
+    nc = tc.nc
+    with ExitStack() as ctx:
+        keep = ctx.enter_context(tc.tile_pool(name="keep", bufs=1))
+        ring = ctx.enter_context(tc.tile_pool(name="ring", bufs=3))
+        psum = ctx.enter_context(tc.psum_pool(name="psum", bufs=2))
+
+        def load_scale_rows(plane, rows):
+            for q in range(4):
+                nc.sync.dma_start(plane[32 * q : 32 * q + 4, :].bitcast(I32), rows[0, 4 * q : 4 * q + 4, :].bitcast(I32))
+
+        def words_of(packed):
+            return packed[0].rearrange("p c i -> p (c i)").bitcast(I32)
+
+        src = keep.tile([P, J // 16], U16, name="src")
+        tgt = keep.tile([P, J // 16], U16, name="tgt")
+        nc.sync.dma_start(src[:], offs)
+        nc.sync.dma_start(tgt[:], offs2)
+        tab_codes = keep.tile([P, T], I32, name="tab_codes", align_bytes=64)
+        nc.sync.dma_start(tab_codes[:], words_of(tab_words))
+
+        tab_plane = keep.tile([P, T], U8, name="tab_plane", align_bytes=64)
+        w_planes = keep.tile([P, 2, N], U8, name="w_planes", align_bytes=64)
+        nc.gpsimd.memset(tab_plane[:].bitcast(I32), 0)
+        nc.gpsimd.memset(w_planes[:].rearrange("p w n -> p (w n)").bitcast(I32), 0)
+        load_scale_rows(tab_plane, tab_scales)
+
+        wb_raw = keep.tile([P, PACK, N], F32, name="wb_raw", tag="wb_then_bytes", align_bytes=64)
+        nc.sync.dma_start(wb_raw[:], wb.rearrange("(p i) n -> p i n", i=PACK))
+        wa_codes = keep.tile([P, N], I32, name="wa_codes", align_bytes=64)
+        wc_codes = keep.tile([P, N], I32, name="wc_codes", align_bytes=64)
+        nc.sync.dma_start(wc_codes[:], words_of(wc_words))
+        nc.sync.dma_start(wa_codes[:], words_of(wa_words))
+        load_scale_rows(w_planes[:, 1, :], wc_scales)
+        load_scale_rows(w_planes[:, 0, :], wa_scales)
+        r_rows = rT.rearrange("(p i) t -> p i t", i=PACK)
+        r_all = []
+        for i in range(PACK):
+            r_i = keep.tile([P, T], F32, name="r_all%d" % i, tag="r_all%d" % i)
+            nc.sync.dma_start(r_i[:], r_rows[:, i, :])
+            r_all.append(r_i)
+        edge_w = keep.tile([P, J], F32, name="edge_w")
+        nc.sync.dma_start(edge_w[:], wgo)
+
+        ident = keep.tile([P, P], F32, name="ident")
+        make_identity(nc, ident[:])
+        warm = keep.tile([P, 1], F32, name="warm")
+        nc.scalar.activation(warm[:], ident[:, 0:1], SIGMOID)
+
+        def gather_table(words, plane, h):
+            cols = slice(h * HALF // 16, (h + 1) * HALF // 16)
+            for side, lst in ((SRC, src), (TGT, tgt)):
+                nc.vector.tensor_copy(words[:, side, :], tab_codes[:].bitcast(U32).indirect(lst[:, cols]))
+            for side, lst in ((SRC, src), (TGT, tgt)):
+                nc.vector.tensor_copy(plane[:, side, :], tab_plane[:].indirect(lst[:, cols]))
+
+        words0 = keep.tile([P, 2, HALF], U32, name="words0", align_bytes=64)
+        plane0 = keep.tile([P, 2, HALF], U8, name="plane0", align_bytes=64)
+        gather_table(words0, plane0, 0)
+
+        wb_bf = keep.tile([P, N, PACK], BF16, name="wb_bf", tag="wb_then_words", align_bytes=64)
+        nc.scalar.copy(
+            wb_bf[:].rearrange("p (c e) i -> p c i e", e=4), wb_raw[:].rearrange("p i (c e) -> p c i e", e=4)
+        )
+        wb_codes = keep.tile([P, N], U32, name="wb_codes", align_bytes=64)
+        wb_plane = keep.tile([P, N], U8, name="wb_plane", align_bytes=64)
+        nc.vector.quantize_mx(wb_codes[:].bitcast(FP8X4), wb_plane[:], wb_bf[:].rearrange("p n i -> p (n i)"))
+
+        words1 = keep.tile([P, 2, HALF], U32, name="words1", tag="wb_then_words", align_bytes=64)
+        plane1 = keep.tile([P, 2, HALF], U8, name="plane1", tag="wb_then_bytes", align_bytes=64)
+        gather_table(words1, plane1, 1)
+        picked = [(words0, plane0), (words1, plane1)]
+
+        gated = []
+        for c in range(CHUNKS):
+            words, plane = picked[c // PER_BANK]
+            in_half = slice((c % PER_BANK) * P, (c % PER_BANK + 1) * P)
+            src_op = dict(lhsT=words[:, SRC, in_half].bitcast(FP8X4), lhsT_scale=plane[:, SRC, in_half])
+            tgt_op = dict(lhsT=words[:, TGT, in_half].bitcast(FP8X4), lhsT_scale=plane[:, TGT, in_half])
+            ms = psum.tile([P, N], F32, name="ms")
+            za = psum.tile([P, N], F32, name="za")
+            nc.tensor.matmul_mx(ms[:], rhs=wc_codes[:].bitcast(FP8X4), rhs_scale=w_planes[:, 1, :], start=True, stop=True, **src_op)
+            nc.tensor.matmul_mx(za[:], rhs=wa_codes[:].bitcast(FP8X4), rhs_scale=w_planes[:, 0, :], start=True, stop=False, **tgt_op)
+            nc.tensor.matmul_mx(za[:], rhs=wb_codes[:].bitcast(FP8X4), rhs_scale=wb_plane[:], start=False, stop=True, **src_op)
+            eta = ring.tile([P, PACK, P], F32, name="eta")
+            nc.scalar.activation(eta[:], za[:].rearrange("j (m i) -> j i m", i=PACK), SIGMOID)
+            if c % 2 == 0:
+                pair = keep.tile([P, 2, PACK, P], F32, name="gated%d" % (c // 2), tag="gated_then_pairs%d" % (c // 2), align_bytes=64)
+            g = pair[:, c % 2, :, :]
+            msg = ring.tile([P, PACK, P], F32, name="msg")
+            nc.scalar.copy(msg[:], ms[:].rearrange("j (m i) -> j i m", i=PACK))
+            nc.gpsimd.tensor_tensor(g, msg[:], eta[:], MULT)
+            gated.append(g)
+
+        r_picked = []
+        for i in range(PACK):
+            r_i = keep.tile([P, J], F32, name="r_picked%d" % i)
+            nc.vector.tensor_copy(r_i[:], r_all[i][:].indirect(tgt[:]))
+            r_picked.append(r_i)
+
+        pages = []
+        for i in range(PACK):
+            if i < 2:
+                page = keep.tile([P, T], F32, name="page%d" % i)
+                nc.vector.memset(page[:], 0.0)
+            else:
+                page = keep.tile([P, T], F32, name="page%d" % i, tag="r_all%d" % i)
+                nc.gpsimd.memset(page[:], 0.0)
+            pages.append(page)
+
+        sums = []
+        for i in range(PACK):
+            summed = keep.tile([P, J], F32, name="summed%d" % i)
+            r_by_edge = []
+            for h in range(2):
+                turned = psum.tile([P, PER_BANK, P], F32, name="turned")
+                for b in range(PER_BANK):
+                    c = h * PER_BANK + b
+                    nc.tensor.transpose(turned[:, b, :], r_picked[i][:, c * P : (c + 1) * P], ident[:])
+                r_ih = keep.tile([P, PER_BANK, P], F32, name="r_by_edge%d_%d" % (i, h))
+                nc.scalar.copy(r_ih[:], turned[:])
+                r_by_edge.append(r_ih)
+            for h in range(2):
+                back = psum.tile([P, PER_BANK, P], F32, name="back")
+                for b in range(PER_BANK):
+                    c = h * PER_BANK + b
+                    nc.tensor.matmul(back[:, b, :], r_by_edge[h][:, b, :], ident[:], start=True, stop=False, is_transpose=True)
+                    nc.tensor.matmul(back[:, b, :], gated[c][:, i, :], ident[:], start=False, stop=True, is_transpose=True)
+                nc.scalar.copy(summed[:, h * HALF : (h + 1) * HALF], back[:].rearrange("p b j -> p (b j)"))
+            sums.append(summed)
+
+        out_rows = out_0.rearrange("(p i) t -> p i t", i=PACK)
+        pairs = [
+            keep.tile([P, 2, QCOLS, 2], BF16, name="pairs%d" % q, tag="gated_then_pairs%d" % q, align_bytes=64)
+            for q in range(PIECES)
+        ]
+        for i in range(PACK):
+            step = HALF if i == 0 else J
+            for j0 in range(0, J, step):
+                edges = slice(j0, j0 + step)
+                nc.vector.tensor_tensor(
+                    pages[i][:].indirect(tgt[:, j0 // 16 : (j0 + step) // 16]), sums[i][:, edges], edge_w[:, edges], MULT
+                )
+            nc.sync.dma_start(out_rows[:, i, :], pages[i][:])
+            for q in range(PIECES):
+                piece = pages[i][:, q * QCOLS : (q + 1) * QCOLS]
+                if i == PACK - 1 and q < VECTOR_PIECES:
+                    nc.vector.tensor_copy(pairs[q][:, i // 2, :, i % 2], piece)
+                elif i == PACK - 2 and q < VECTOR_PIECES:
+                    nc.scalar.copy(pairs[q][:, i // 2, :, :], piece.unsqueeze(2).to_broadcast([P, QCOLS, 2]))
+                else:
+                    nc.scalar.copy(pairs[q][:, i // 2, :, i % 2], piece)
+
+        woven = [keep.tile([P, QCOLS * PACK], BF16, name="woven%d" % q, align_bytes=64) for q in range(PIECES)]
+        for q in range(PIECES):
+            word = I32 if q < VECTOR_PIECES else U32
+            dst = woven[q][:].bitcast(word).rearrange("p (c u) -> p c u", u=2)
+            both = pairs[q][:].rearrange("p u c e -> p (u c e)").bitcast(word).rearrange("p (u c) -> p c u", u=2)
+            if q < VECTOR_PIECES:
+                nc.vector.tensor_copy(dst, both)
+            else:
+                nc.scalar.copy(dst, both)
+
+        out_plane = keep.tile([P, T], U8, name="out_plane", align_bytes=64)
+        out_words = words_of(out_1)
+        for q in range(PIECES):
+            cols = slice(q * QCOLS, (q + 1) * QCOLS)
+            codes = keep.tile([P, QCOLS], I32, name="out_codes%d" % q, align_bytes=64)
+            nc.vector.quantize_mx(codes[:].bitcast(FP8X4), out_plane[:, cols], woven[q][:])
+            nc.sync.dma_start(out_words[:, cols], codes[:])
+        for q in range(4):
+            queue = nc.sync if q % 2 == 0 else nc.scalar
+            queue.dma_start(out_2[0, 4 * q : 4 * q + 4, :].bitcast(I32), out_plane[32 * q : 32 * q + 4, :].bitcast(I32))

@@ -34,8 +34,9 @@ def tile_list_rgg_LP_kernel(
     nc = tc.nc
     with ExitStack() as ctx:
         keep = ctx.enter_context(tc.tile_pool(name="keep", bufs=1))
-        ring = ctx.enter_context(tc.tile_pool(name="ring", bufs=3))
-        psum = ctx.enter_context(tc.psum_pool(name="psum", bufs=2))
+        ring = ctx.enter_context(tc.tile_pool(name="ring", bufs=6))
+        reuse = ctx.enter_context(tc.tile_pool(name="reuse", bufs=1))
+        psum = ctx.enter_context(tc.psum_pool(name="psum", bufs=8))
 
         def load_scale_rows(plane, rows):
             for q in range(4):
@@ -57,7 +58,7 @@ def tile_list_rgg_LP_kernel(
         nc.gpsimd.memset(w_planes[:].rearrange("p w n -> p (w n)").bitcast(I32), 0)
         load_scale_rows(tab_plane, tab_scales)
 
-        wb_raw = keep.tile([P, PACK, N], F32, name="wb_raw", tag="wb_then_bytes", align_bytes=64)
+        wb_raw = keep.tile([P, PACK, N], F32, name="wb_raw")
         nc.sync.dma_start(wb_raw[:], wb.rearrange("(p i) n -> p i n", i=PACK))
         wa_codes = keep.tile([P, N], I32, name="wa_codes", align_bytes=64)
         wc_codes = keep.tile([P, N], I32, name="wc_codes", align_bytes=64)
@@ -68,7 +69,7 @@ def tile_list_rgg_LP_kernel(
         r_rows = rT.rearrange("(p i) t -> p i t", i=PACK)
         r_all = []
         for i in range(PACK):
-            r_i = keep.tile([P, T], F32, name="r_all%d" % i, tag="r_all%d" % i)
+            r_i = keep.tile([P, T], F32, name="r_all%d" % i)
             nc.sync.dma_start(r_i[:], r_rows[:, i, :])
             r_all.append(r_i)
         edge_w = keep.tile([P, J], F32, name="edge_w")
@@ -76,8 +77,18 @@ def tile_list_rgg_LP_kernel(
 
         ident = keep.tile([P, P], F32, name="ident")
         make_identity(nc, ident[:])
+        pages = []
+        for i in range(PACK):
+            if i < 2:
+                page = keep.tile([P, T], F32, name="page%d" % i)
+                nc.vector.memset(page[:], 0.0)
+            else:
+                page = keep.tile([P, T], F32, name="page%d" % i)
+                nc.gpsimd.memset(page[:], 0.0)
+            pages.append(page)
+
         warm = keep.tile([P, 1], F32, name="warm")
-        nc.scalar.activation(warm[:], ident[:, 0:1], SIGMOID)
+        nc.scalar.activation(warm[:], pages[0][:, 0:1], SIGMOID)
 
         def gather_table(words, plane, h):
             cols = slice(h * HALF // 16, (h + 1) * HALF // 16)
@@ -90,7 +101,7 @@ def tile_list_rgg_LP_kernel(
         plane0 = keep.tile([P, 2, HALF], U8, name="plane0", align_bytes=64)
         gather_table(words0, plane0, 0)
 
-        wb_bf = keep.tile([P, N, PACK], BF16, name="wb_bf", tag="wb_then_words", align_bytes=64)
+        wb_bf = reuse.tile([P, N, PACK], BF16, name="wb_bf", align_bytes=64, offset=0)
         nc.scalar.copy(
             wb_bf[:].rearrange("p (c e) i -> p c i e", e=4), wb_raw[:].rearrange("p i (c e) -> p c i e", e=4)
         )
@@ -98,8 +109,8 @@ def tile_list_rgg_LP_kernel(
         wb_plane = keep.tile([P, N], U8, name="wb_plane", align_bytes=64)
         nc.vector.quantize_mx(wb_codes[:].bitcast(FP8X4), wb_plane[:], wb_bf[:].rearrange("p n i -> p (n i)"))
 
-        words1 = keep.tile([P, 2, HALF], U32, name="words1", tag="wb_then_words", align_bytes=64)
-        plane1 = keep.tile([P, 2, HALF], U8, name="plane1", tag="wb_then_bytes", align_bytes=64)
+        words1 = reuse.tile([P, 2, HALF], U32, name="words1", align_bytes=64, offset=2 * HALF)
+        plane1 = reuse.tile([P, 2, HALF], U8, name="plane1", align_bytes=64, offset=0)
         gather_table(words1, plane1, 1)
         picked = [(words0, plane0), (words1, plane1)]
 
@@ -109,8 +120,8 @@ def tile_list_rgg_LP_kernel(
             in_half = slice((c % PER_BANK) * P, (c % PER_BANK + 1) * P)
             src_op = dict(lhsT=words[:, SRC, in_half].bitcast(FP8X4), lhsT_scale=plane[:, SRC, in_half])
             tgt_op = dict(lhsT=words[:, TGT, in_half].bitcast(FP8X4), lhsT_scale=plane[:, TGT, in_half])
-            ms = psum.tile([P, N], F32, name="ms")
-            za = psum.tile([P, N], F32, name="za")
+            ms = psum.tile([P, N], F32, name="ms", tag="bank")
+            za = psum.tile([P, N], F32, name="za", tag="bank")
             nc.tensor.matmul_mx(ms[:], rhs=wc_codes[:].bitcast(FP8X4), rhs_scale=w_planes[:, 1, :], start=True, stop=True, **src_op)
             nc.tensor.matmul_mx(za[:], rhs=wa_codes[:].bitcast(FP8X4), rhs_scale=w_planes[:, 0, :], start=True, stop=False, **tgt_op)
             nc.tensor.matmul_mx(za[:], rhs=wb_codes[:].bitcast(FP8X4), rhs_scale=wb_plane[:], start=False, stop=True, **src_op)
@@ -130,22 +141,12 @@ def tile_list_rgg_LP_kernel(
             nc.vector.tensor_copy(r_i[:], r_all[i][:].indirect(tgt[:]))
             r_picked.append(r_i)
 
-        pages = []
-        for i in range(PACK):
-            if i < 2:
-                page = keep.tile([P, T], F32, name="page%d" % i)
-                nc.vector.memset(page[:], 0.0)
-            else:
-                page = keep.tile([P, T], F32, name="page%d" % i, tag="r_all%d" % i)
-                nc.gpsimd.memset(page[:], 0.0)
-            pages.append(page)
-
         sums = []
         for i in range(PACK):
             summed = keep.tile([P, J], F32, name="summed%d" % i)
             r_by_edge = []
             for h in range(2):
-                turned = psum.tile([P, PER_BANK, P], F32, name="turned")
+                turned = psum.tile([P, PER_BANK, P], F32, name="turned", tag="bank")
                 for b in range(PER_BANK):
                     c = h * PER_BANK + b
                     nc.tensor.transpose(turned[:, b, :], r_picked[i][:, c * P : (c + 1) * P], ident[:])
@@ -153,7 +154,7 @@ def tile_list_rgg_LP_kernel(
                 nc.scalar.copy(r_ih[:], turned[:])
                 r_by_edge.append(r_ih)
             for h in range(2):
-                back = psum.tile([P, PER_BANK, P], F32, name="back")
+                back = psum.tile([P, PER_BANK, P], F32, name="back", tag="bank")
                 for b in range(PER_BANK):
                     c = h * PER_BANK + b
                     nc.tensor.matmul(back[:, b, :], r_by_edge[h][:, b, :], ident[:], start=True, stop=False, is_transpose=True)

@@ -18,14 +18,19 @@ SIGMOID = mybir.ActivationFunctionType.Sigmoid
 
 P = 128
 PACK = 4
+QUADRANTS = 4
+LIST_ROWS = 16
 HALF = J // 2
 CHUNKS = J // P
-BANK = 512
-PER_BANK = BANK // P
-QCOLS = 512
-PIECES = T // QCOLS
+PER_HALF = HALF // P
+EARLY_PAGES = 2
+PIECE = 512
+PIECES = T // PIECE
 VECTOR_PIECES = 2
+RING = 6
+SHARED_BANKS = 6
 SRC, TGT = 0, 1
+WA, WC = 0, 1
 
 
 def tile_list_rgg_LP_kernel(
@@ -34,44 +39,58 @@ def tile_list_rgg_LP_kernel(
     nc = tc.nc
     with ExitStack() as ctx:
         keep = ctx.enter_context(tc.tile_pool(name="keep", bufs=1))
-        ring = ctx.enter_context(tc.tile_pool(name="ring", bufs=6))
-        reuse = ctx.enter_context(tc.tile_pool(name="reuse", bufs=1))
-        psum = ctx.enter_context(tc.psum_pool(name="psum", bufs=8))
+        ring = ctx.enter_context(tc.tile_pool(name="ring", bufs=RING))
+        psum = ctx.enter_context(tc.psum_pool(name="psum", bufs=SHARED_BANKS))
 
-        def load_scale_rows(plane, rows):
-            for q in range(4):
-                nc.sync.dma_start(plane[32 * q : 32 * q + 4, :].bitcast(I32), rows[0, 4 * q : 4 * q + 4, :].bitcast(I32))
+        def live_rows(plane, quad):
+            return plane[32 * quad : 32 * quad + 4, :].bitcast(I32)
+
+        def scale_rows(scales, quad):
+            return scales[0, 4 * quad : 4 * quad + 4, :].bitcast(I32)
+
+        def load_plane(plane, scales):
+            for quad in range(QUADRANTS):
+                nc.sync.dma_start(live_rows(plane, quad), scale_rows(scales, quad))
 
         def words_of(packed):
             return packed[0].rearrange("p c i -> p (c i)").bitcast(I32)
 
-        src = keep.tile([P, J // 16], U16, name="src")
-        tgt = keep.tile([P, J // 16], U16, name="tgt")
+        def entries(lst, first, count):
+            return lst[:, first // LIST_ROWS : (first + count) // LIST_ROWS]
+
+        src = keep.tile([P, J // LIST_ROWS], U16, name="src")
+        tgt = keep.tile([P, J // LIST_ROWS], U16, name="tgt")
         nc.sync.dma_start(src[:], offs)
         nc.sync.dma_start(tgt[:], offs2)
-        tab_codes = keep.tile([P, T], I32, name="tab_codes", align_bytes=64)
-        nc.sync.dma_start(tab_codes[:], words_of(tab_words))
+        lists = ((SRC, src), (TGT, tgt))
 
         tab_plane = keep.tile([P, T], U8, name="tab_plane", align_bytes=64)
         w_planes = keep.tile([P, 2, N], U8, name="w_planes", align_bytes=64)
         nc.gpsimd.memset(tab_plane[:].bitcast(I32), 0)
         nc.gpsimd.memset(w_planes[:].rearrange("p w n -> p (w n)").bitcast(I32), 0)
-        load_scale_rows(tab_plane, tab_scales)
+        load_plane(tab_plane, tab_scales)
+        tab_codes = keep.tile([P, T], I32, name="tab_codes", align_bytes=64)
+        nc.sync.dma_start(tab_codes[:], words_of(tab_words))
 
-        wb_raw = keep.tile([P, PACK, N], F32, name="wb_raw")
-        nc.sync.dma_start(wb_raw[:], wb.rearrange("(p i) n -> p i n", i=PACK))
+        wb_rows = wb.rearrange("(p i) n -> p i n", i=PACK)
+        wb_cols = [slice(0, N // 2), slice(N // 2, N)]
+        wb_raw = []
+        for u, cols in enumerate(wb_cols):
+            part = keep.tile([P, PACK, N // 2], F32, name="wb_raw%d" % u)
+            nc.sync.dma_start(part[:], wb_rows[:, :, cols])
+            wb_raw.append(part)
         wa_codes = keep.tile([P, N], I32, name="wa_codes", align_bytes=64)
         wc_codes = keep.tile([P, N], I32, name="wc_codes", align_bytes=64)
         nc.sync.dma_start(wc_codes[:], words_of(wc_words))
         nc.sync.dma_start(wa_codes[:], words_of(wa_words))
-        load_scale_rows(w_planes[:, 1, :], wc_scales)
-        load_scale_rows(w_planes[:, 0, :], wa_scales)
+        load_plane(w_planes[:, WC, :], wc_scales)
+        load_plane(w_planes[:, WA, :], wa_scales)
         r_rows = rT.rearrange("(p i) t -> p i t", i=PACK)
         r_all = []
         for i in range(PACK):
-            r_i = keep.tile([P, T], F32, name="r_all%d" % i)
-            nc.sync.dma_start(r_i[:], r_rows[:, i, :])
-            r_all.append(r_i)
+            rows = keep.tile([P, T], F32, name="r_all%d" % i)
+            nc.sync.dma_start(rows[:], r_rows[:, i, :])
+            r_all.append(rows)
         edge_w = keep.tile([P, J], F32, name="edge_w")
         nc.sync.dma_start(edge_w[:], wgo)
 
@@ -79,128 +98,157 @@ def tile_list_rgg_LP_kernel(
         make_identity(nc, ident[:])
         pages = []
         for i in range(PACK):
-            if i < 2:
-                page = keep.tile([P, T], F32, name="page%d" % i)
-                nc.vector.memset(page[:], 0.0)
-            else:
-                page = keep.tile([P, T], F32, name="page%d" % i)
-                nc.gpsimd.memset(page[:], 0.0)
+            page = keep.tile([P, T], F32, name="page%d" % i)
+            engine = nc.vector if i == 0 else nc.gpsimd
+            engine.memset(page[:], 0.0)
             pages.append(page)
 
-        warm = keep.tile([P, 1], F32, name="warm")
-        nc.scalar.activation(warm[:], pages[0][:, 0:1], SIGMOID)
+        picked_plane = keep.tile([P, 2, J], U8, name="picked_plane", align_bytes=64)
+        for side, lst in lists:
+            nc.vector.tensor_copy(picked_plane[:, side, :], tab_plane[:].indirect(lst[:]))
 
-        def gather_table(words, plane, h):
-            cols = slice(h * HALF // 16, (h + 1) * HALF // 16)
-            for side, lst in ((SRC, src), (TGT, tgt)):
-                nc.vector.tensor_copy(words[:, side, :], tab_codes[:].bitcast(U32).indirect(lst[:, cols]))
-            for side, lst in ((SRC, src), (TGT, tgt)):
-                nc.vector.tensor_copy(plane[:, side, :], tab_plane[:].indirect(lst[:, cols]))
+        def gather_words(words, h):
+            for side, lst in lists:
+                window = tab_codes[:].bitcast(U32)
+                nc.vector.tensor_copy(words[:, side, :], window.indirect(entries(lst, h * HALF, HALF)))
 
         words0 = keep.tile([P, 2, HALF], U32, name="words0", align_bytes=64)
-        plane0 = keep.tile([P, 2, HALF], U8, name="plane0", align_bytes=64)
-        gather_table(words0, plane0, 0)
+        gather_words(words0, 0)
 
-        wb_bf = reuse.tile([P, N, PACK], BF16, name="wb_bf", align_bytes=64, offset=0)
-        nc.scalar.copy(
-            wb_bf[:].rearrange("p (c e) i -> p c i e", e=4), wb_raw[:].rearrange("p i (c e) -> p c i e", e=4)
-        )
+        wb_bf = keep.tile([P, N, PACK], BF16, name="wb_bf", tag="wb_then_words", align_bytes=64)
+        for part, cols in zip(wb_raw, wb_cols):
+            nc.scalar.copy(
+                wb_bf[:, cols, :].rearrange("p (c e) i -> p c i e", e=4),
+                part[:].rearrange("p i (c e) -> p c i e", e=4),
+            )
         wb_codes = keep.tile([P, N], U32, name="wb_codes", align_bytes=64)
         wb_plane = keep.tile([P, N], U8, name="wb_plane", align_bytes=64)
         nc.vector.quantize_mx(wb_codes[:].bitcast(FP8X4), wb_plane[:], wb_bf[:].rearrange("p n i -> p (n i)"))
 
-        words1 = reuse.tile([P, 2, HALF], U32, name="words1", align_bytes=64, offset=2 * HALF)
-        plane1 = reuse.tile([P, 2, HALF], U8, name="plane1", align_bytes=64, offset=0)
-        gather_table(words1, plane1, 1)
-        picked = [(words0, plane0), (words1, plane1)]
+        words1 = keep.tile([P, 2, HALF], U32, name="words1", tag="wb_then_words", align_bytes=64)
+        gather_words(words1, 1)
+        picked_words = [words0, words1]
 
         gated = []
         for c in range(CHUNKS):
-            words, plane = picked[c // PER_BANK]
-            in_half = slice((c % PER_BANK) * P, (c % PER_BANK + 1) * P)
-            src_op = dict(lhsT=words[:, SRC, in_half].bitcast(FP8X4), lhsT_scale=plane[:, SRC, in_half])
-            tgt_op = dict(lhsT=words[:, TGT, in_half].bitcast(FP8X4), lhsT_scale=plane[:, TGT, in_half])
+            words = picked_words[c // PER_HALF]
+            edges = slice(c * P, (c + 1) * P)
+            in_half = slice((c % PER_HALF) * P, (c % PER_HALF + 1) * P)
+            src_op = dict(lhsT=words[:, SRC, in_half].bitcast(FP8X4), lhsT_scale=picked_plane[:, SRC, edges])
+            tgt_op = dict(lhsT=words[:, TGT, in_half].bitcast(FP8X4), lhsT_scale=picked_plane[:, TGT, edges])
+            wa_op = dict(rhs=wa_codes[:].bitcast(FP8X4), rhs_scale=w_planes[:, WA, :])
+            wb_op = dict(rhs=wb_codes[:].bitcast(FP8X4), rhs_scale=wb_plane[:])
+            wc_op = dict(rhs=wc_codes[:].bitcast(FP8X4), rhs_scale=w_planes[:, WC, :])
             ms = psum.tile([P, N], F32, name="ms", tag="bank")
             za = psum.tile([P, N], F32, name="za", tag="bank")
-            nc.tensor.matmul_mx(ms[:], rhs=wc_codes[:].bitcast(FP8X4), rhs_scale=w_planes[:, 1, :], start=True, stop=True, **src_op)
-            nc.tensor.matmul_mx(za[:], rhs=wa_codes[:].bitcast(FP8X4), rhs_scale=w_planes[:, 0, :], start=True, stop=False, **tgt_op)
-            nc.tensor.matmul_mx(za[:], rhs=wb_codes[:].bitcast(FP8X4), rhs_scale=wb_plane[:], start=False, stop=True, **src_op)
+            nc.tensor.matmul_mx(ms[:], start=True, stop=True, **src_op, **wc_op)
+            nc.tensor.matmul_mx(za[:], start=True, stop=False, **tgt_op, **wa_op)
+            nc.tensor.matmul_mx(za[:], start=False, stop=True, **src_op, **wb_op)
             eta = ring.tile([P, PACK, P], F32, name="eta")
             nc.scalar.activation(eta[:], za[:].rearrange("j (m i) -> j i m", i=PACK), SIGMOID)
             if c % 2 == 0:
-                pair = keep.tile([P, 2, PACK, P], F32, name="gated%d" % (c // 2), tag="gated_then_pairs%d" % (c // 2), align_bytes=64)
-            g = pair[:, c % 2, :, :]
+                two_chunks = keep.tile(
+                    [P, 2, PACK, P], F32, name="gated%d" % (c // 2), tag="gated_then_pairs%d" % (c // 2), align_bytes=64
+                )
+            product = two_chunks[:, c % 2, :, :]
             msg = ring.tile([P, PACK, P], F32, name="msg")
             nc.scalar.copy(msg[:], ms[:].rearrange("j (m i) -> j i m", i=PACK))
-            nc.gpsimd.tensor_tensor(g, msg[:], eta[:], MULT)
-            gated.append(g)
+            nc.gpsimd.tensor_tensor(product, msg[:], eta[:], MULT)
+            gated.append(product)
 
         r_picked = []
         for i in range(PACK):
-            r_i = keep.tile([P, J], F32, name="r_picked%d" % i)
-            nc.vector.tensor_copy(r_i[:], r_all[i][:].indirect(tgt[:]))
-            r_picked.append(r_i)
+            rows = keep.tile([P, J], F32, name="r_picked%d" % i)
+            nc.vector.tensor_copy(rows[:], r_all[i][:].indirect(tgt[:]))
+            r_picked.append(rows)
 
-        sums = []
-        for i in range(PACK):
-            summed = keep.tile([P, J], F32, name="summed%d" % i)
-            r_by_edge = []
+        def transposed_bank(first_sum_bank):
+            if first_sum_bank is None:
+                return psum.tile([P, PER_HALF, P], F32, name="turned", tag="bank")
+            return psum.tile([P, PER_HALF, P], F32, name="turned", tag="first_sum%d" % first_sum_bank, bufs=1)
+
+        r_by_edge = {}
+
+        def turn_r(i):
             for h in range(2):
-                turned = psum.tile([P, PER_BANK, P], F32, name="turned", tag="bank")
-                for b in range(PER_BANK):
-                    c = h * PER_BANK + b
-                    nc.tensor.transpose(turned[:, b, :], r_picked[i][:, c * P : (c + 1) * P], ident[:])
-                r_ih = keep.tile([P, PER_BANK, P], F32, name="r_by_edge%d_%d" % (i, h))
-                nc.scalar.copy(r_ih[:], turned[:])
-                r_by_edge.append(r_ih)
+                bank = transposed_bank(h if i >= EARLY_PAGES else None)
+                for b in range(PER_HALF):
+                    c = h * PER_HALF + b
+                    nc.tensor.transpose(bank[:, b, :], r_picked[i][:, c * P : (c + 1) * P], ident[:])
+                turned = keep.tile([P, PER_HALF, P], F32, name="r_by_edge%d_%d" % (i, h))
+                nc.scalar.copy(turned[:], bank[:])
+                r_by_edge[i, h] = turned
+
+        sums = [keep.tile([P, J], F32, name="sums%d" % i) for i in range(PACK)]
+
+        def add_and_turn_back(i, h):
+            bank = transposed_bank(i if h == 0 and i < EARLY_PAGES else None)
+            for b in range(PER_HALF):
+                terms = (r_by_edge[i, h][:, b, :], gated[h * PER_HALF + b][:, i, :])
+                for term, first in zip(terms, (True, False)):
+                    nc.tensor.matmul(bank[:, b, :], term, ident[:], start=first, stop=not first, is_transpose=True)
+            nc.scalar.copy(sums[i][:, h * HALF : (h + 1) * HALF], bank[:].rearrange("p b j -> p (b j)"))
+
+        for i in range(EARLY_PAGES):
+            turn_r(i)
+        for h in range(2):
+            for i in range(EARLY_PAGES):
+                add_and_turn_back(i, h)
+            turn_r(EARLY_PAGES + h)
+        for i in range(EARLY_PAGES, PACK):
             for h in range(2):
-                back = psum.tile([P, PER_BANK, P], F32, name="back", tag="bank")
-                for b in range(PER_BANK):
-                    c = h * PER_BANK + b
-                    nc.tensor.matmul(back[:, b, :], r_by_edge[h][:, b, :], ident[:], start=True, stop=False, is_transpose=True)
-                    nc.tensor.matmul(back[:, b, :], gated[c][:, i, :], ident[:], start=False, stop=True, is_transpose=True)
-                nc.scalar.copy(summed[:, h * HALF : (h + 1) * HALF], back[:].rearrange("p b j -> p (b j)"))
-            sums.append(summed)
+                add_and_turn_back(i, h)
 
         out_rows = out_0.rearrange("(p i) t -> p i t", i=PACK)
         pairs = [
-            keep.tile([P, 2, QCOLS, 2], BF16, name="pairs%d" % q, tag="gated_then_pairs%d" % q, align_bytes=64)
+            keep.tile([P, 2, PIECE, 2], BF16, name="pairs%d" % q, tag="gated_then_pairs%d" % q, align_bytes=64)
             for q in range(PIECES)
         ]
+
+        def scatter(i, first, count):
+            edges = slice(first, first + count)
+            places = pages[i][:].indirect(entries(tgt, first, count))
+            nc.vector.tensor_tensor(places, sums[i][:, edges], edge_w[:, edges], MULT)
+
+        for i in range(EARLY_PAGES):
+            scatter(i, 0, HALF)
         for i in range(PACK):
-            step = HALF if i == 0 else J
-            for j0 in range(0, J, step):
-                edges = slice(j0, j0 + step)
-                nc.vector.tensor_tensor(
-                    pages[i][:].indirect(tgt[:, j0 // 16 : (j0 + step) // 16]), sums[i][:, edges], edge_w[:, edges], MULT
-                )
+            if i < EARLY_PAGES:
+                scatter(i, HALF, HALF)
+            else:
+                scatter(i, 0, J)
             nc.sync.dma_start(out_rows[:, i, :], pages[i][:])
             for q in range(PIECES):
-                piece = pages[i][:, q * QCOLS : (q + 1) * QCOLS]
+                piece = pages[i][:, q * PIECE : (q + 1) * PIECE]
                 if i == PACK - 1 and q < VECTOR_PIECES:
                     nc.vector.tensor_copy(pairs[q][:, i // 2, :, i % 2], piece)
                 elif i == PACK - 2 and q < VECTOR_PIECES:
-                    nc.scalar.copy(pairs[q][:, i // 2, :, :], piece.unsqueeze(2).to_broadcast([P, QCOLS, 2]))
+                    nc.scalar.copy(pairs[q][:, i // 2, :, :], piece.unsqueeze(2).to_broadcast([P, PIECE, 2]))
                 else:
                     nc.scalar.copy(pairs[q][:, i // 2, :, i % 2], piece)
 
-        woven = [keep.tile([P, QCOLS * PACK], BF16, name="woven%d" % q, align_bytes=64) for q in range(PIECES)]
-        for q in range(PIECES):
+        last = (PIECES - 1) * PIECE
+        spans = [(q * PIECE, PIECE) for q in range(PIECES - 1)] + [(last, PIECE // 2), (last + PIECE // 2, PIECE // 2)]
+        woven = []
+        for first, width in spans:
+            q, inner = divmod(first, PIECE)
             word = I32 if q < VECTOR_PIECES else U32
-            dst = woven[q][:].bitcast(word).rearrange("p (c u) -> p c u", u=2)
+            span = keep.tile([P, width * PACK], BF16, name="woven%d" % first, align_bytes=64)
+            dst = span[:].bitcast(word).rearrange("p (c u) -> p c u", u=2)
             both = pairs[q][:].rearrange("p u c e -> p (u c e)").bitcast(word).rearrange("p (u c) -> p c u", u=2)
             if q < VECTOR_PIECES:
-                nc.vector.tensor_copy(dst, both)
+                nc.vector.tensor_copy(dst, both[:, inner : inner + width, :])
             else:
-                nc.scalar.copy(dst, both)
+                nc.scalar.copy(dst, both[:, inner : inner + width, :])
+            woven.append(span)
 
         out_plane = keep.tile([P, T], U8, name="out_plane", align_bytes=64)
+        out_codes = keep.tile([P, T], I32, name="out_codes", align_bytes=64)
         out_words = words_of(out_1)
-        for q in range(PIECES):
-            cols = slice(q * QCOLS, (q + 1) * QCOLS)
-            codes = keep.tile([P, QCOLS], I32, name="out_codes%d" % q, align_bytes=64)
-            nc.vector.quantize_mx(codes[:].bitcast(FP8X4), out_plane[:, cols], woven[q][:])
-            nc.sync.dma_start(out_words[:, cols], codes[:])
-        for q in range(4):
-            queue = nc.sync if q % 2 == 0 else nc.scalar
-            queue.dma_start(out_2[0, 4 * q : 4 * q + 4, :].bitcast(I32), out_plane[32 * q : 32 * q + 4, :].bitcast(I32))
+        for (first, width), span in zip(spans, woven):
+            cols = slice(first, first + width)
+            nc.vector.quantize_mx(out_codes[:, cols].bitcast(FP8X4), out_plane[:, cols], span[:])
+            nc.sync.dma_start(out_words[:, cols], out_codes[:, cols])
+        for quad in range(QUADRANTS):
+            queue = nc.sync if quad % 2 == 0 else nc.scalar
+            queue.dma_start(scale_rows(out_2, quad), live_rows(out_plane, quad))

@@ -24,6 +24,7 @@ HALF = J // 2
 CHUNKS = J // P
 PER_HALF = HALF // P
 EARLY_PAGES = 2
+LATE_CHUNKS = 2
 PIECE = 512
 PIECES = T // PIECE
 VECTOR_PIECES = 2
@@ -129,8 +130,13 @@ def tile_list_rgg_LP_kernel(
         gather_words(words1, 1)
         picked_words = [words0, words1]
 
-        gated = []
-        for c in range(CHUNKS):
+        two_chunks = [
+            keep.tile([P, 2, PACK, P], F32, name="gated%d" % q, tag="gated_then_pairs%d" % q, align_bytes=64)
+            for q in range(CHUNKS // 2)
+        ]
+        gated = [two_chunks[c // 2][:, c % 2, :, :] for c in range(CHUNKS)]
+
+        def gate(c):
             words = picked_words[c // PER_HALF]
             edges = slice(c * P, (c + 1) * P)
             in_half = slice((c % PER_HALF) * P, (c % PER_HALF + 1) * P)
@@ -146,15 +152,12 @@ def tile_list_rgg_LP_kernel(
             nc.tensor.matmul_mx(za[:], start=False, stop=True, **src_op, **wb_op)
             eta = ring.tile([P, PACK, P], F32, name="eta")
             nc.scalar.activation(eta[:], za[:].rearrange("j (m i) -> j i m", i=PACK), SIGMOID)
-            if c % 2 == 0:
-                two_chunks = keep.tile(
-                    [P, 2, PACK, P], F32, name="gated%d" % (c // 2), tag="gated_then_pairs%d" % (c // 2), align_bytes=64
-                )
-            product = two_chunks[:, c % 2, :, :]
             msg = ring.tile([P, PACK, P], F32, name="msg")
             nc.scalar.copy(msg[:], ms[:].rearrange("j (m i) -> j i m", i=PACK))
-            nc.gpsimd.tensor_tensor(product, msg[:], eta[:], MULT)
-            gated.append(product)
+            nc.gpsimd.tensor_tensor(gated[c], msg[:], eta[:], MULT)
+
+        for c in range(CHUNKS - LATE_CHUNKS):
+            gate(c)
 
         r_picked = []
         for i in range(PACK):
@@ -169,15 +172,14 @@ def tile_list_rgg_LP_kernel(
 
         r_by_edge = {}
 
-        def turn_r(i):
-            for h in range(2):
-                bank = transposed_bank(h if i >= EARLY_PAGES else None)
-                for b in range(PER_HALF):
-                    c = h * PER_HALF + b
-                    nc.tensor.transpose(bank[:, b, :], r_picked[i][:, c * P : (c + 1) * P], ident[:])
-                turned = keep.tile([P, PER_HALF, P], F32, name="r_by_edge%d_%d" % (i, h))
-                nc.scalar.copy(turned[:], bank[:])
-                r_by_edge[i, h] = turned
+        def turn_r(i, h, first_sum_bank):
+            bank = transposed_bank(first_sum_bank)
+            for b in range(PER_HALF):
+                c = h * PER_HALF + b
+                nc.tensor.transpose(bank[:, b, :], r_picked[i][:, c * P : (c + 1) * P], ident[:])
+            turned = keep.tile([P, PER_HALF, P], F32, name="r_by_edge%d_%d" % (i, h))
+            nc.scalar.copy(turned[:], bank[:])
+            r_by_edge[i, h] = turned
 
         sums = [keep.tile([P, J], F32, name="sums%d" % i) for i in range(PACK)]
 
@@ -189,13 +191,18 @@ def tile_list_rgg_LP_kernel(
                     nc.tensor.matmul(bank[:, b, :], term, ident[:], start=first, stop=not first, is_transpose=True)
             nc.scalar.copy(sums[i][:, h * HALF : (h + 1) * HALF], bank[:].rearrange("p b j -> p (b j)"))
 
+        turn_r(0, 0, 1)
+        add_and_turn_back(0, 0)
+        for c in range(CHUNKS - LATE_CHUNKS, CHUNKS):
+            gate(c)
+        turn_r(1, 0, None)
+        add_and_turn_back(1, 0)
         for i in range(EARLY_PAGES):
-            turn_r(i)
-        for h in range(2):
-            for i in range(EARLY_PAGES):
-                add_and_turn_back(i, h)
-            turn_r(EARLY_PAGES + h)
+            turn_r(i, 1, None)
+            add_and_turn_back(i, 1)
         for i in range(EARLY_PAGES, PACK):
+            for h in range(2):
+                turn_r(i, h, h)
             for h in range(2):
                 add_and_turn_back(i, h)
 

@@ -14,6 +14,8 @@ U16 = mybir.dt.uint16
 U8 = mybir.dt.uint8
 FP8X4 = mybir.dt.float8_e4m3fn_x4
 MULT = mybir.AluOpType.mult
+ADD = mybir.AluOpType.add
+COPY = mybir.ActivationFunctionType.Copy
 SIGMOID = mybir.ActivationFunctionType.Sigmoid
 
 P = 128
@@ -27,7 +29,10 @@ EARLY_PAGES = 2
 LATE_CHUNKS = 2
 PIECE = 512
 PIECES = T // PIECE
-VECTOR_PIECES = 2
+GPSIMD_PIECES = 2
+SPAN_WIDTHS = (512, 256, 256, 512, 256, 128, 128)
+VECTOR_COLUMNS = 768
+STORE_ENDS = (768, 1536, 2048)
 RING = 6
 SHARED_BANKS = 6
 SRC, TGT = 0, 1
@@ -49,9 +54,9 @@ def tile_list_rgg_LP_kernel(
         def scale_rows(scales, quad):
             return scales[0, 4 * quad : 4 * quad + 4, :].bitcast(I32)
 
-        def load_plane(plane, scales):
+        def load_plane(plane, scales, queues):
             for quad in range(QUADRANTS):
-                nc.sync.dma_start(live_rows(plane, quad), scale_rows(scales, quad))
+                queues[quad % len(queues)].dma_start(live_rows(plane, quad), scale_rows(scales, quad))
 
         def words_of(packed):
             return packed[0].rearrange("p c i -> p (c i)").bitcast(I32)
@@ -62,14 +67,16 @@ def tile_list_rgg_LP_kernel(
         src = keep.tile([P, J // LIST_ROWS], U16, name="src")
         tgt = keep.tile([P, J // LIST_ROWS], U16, name="tgt")
         nc.sync.dma_start(src[:], offs)
-        nc.sync.dma_start(tgt[:], offs2)
-        lists = ((SRC, src), (TGT, tgt))
+        lists = (src, tgt)
 
         tab_plane = keep.tile([P, T], U8, name="tab_plane", align_bytes=64)
         w_planes = keep.tile([P, 2, N], U8, name="w_planes", align_bytes=64)
         nc.gpsimd.memset(tab_plane[:].bitcast(I32), 0)
         nc.gpsimd.memset(w_planes[:].rearrange("p w n -> p (w n)").bitcast(I32), 0)
-        load_plane(tab_plane, tab_scales)
+        w_rows = keep.tile([P, P], F32, name="w_rows")
+        nc.gpsimd.memset(w_rows[:], 0.0)
+        load_plane(tab_plane, tab_scales, (nc.scalar, nc.sync))
+        nc.sync.dma_start(tgt[:], offs2)
         tab_codes = keep.tile([P, T], I32, name="tab_codes", align_bytes=64)
         nc.sync.dma_start(tab_codes[:], words_of(tab_words))
 
@@ -82,66 +89,79 @@ def tile_list_rgg_LP_kernel(
             wb_raw.append(part)
         wa_codes = keep.tile([P, N], I32, name="wa_codes", align_bytes=64)
         wc_codes = keep.tile([P, N], I32, name="wc_codes", align_bytes=64)
+        load_plane(w_planes[:, WC, :], wc_scales, (nc.sync,))
+        nc.sync.dma_start(w_rows[0:CHUNKS, :], wgo[0:1, :].rearrange("o (c j) -> (o c) j", j=P))
         nc.sync.dma_start(wc_codes[:], words_of(wc_words))
         nc.sync.dma_start(wa_codes[:], words_of(wa_words))
-        load_plane(w_planes[:, WC, :], wc_scales)
-        load_plane(w_planes[:, WA, :], wa_scales)
+        load_plane(w_planes[:, WA, :], wa_scales, (nc.gpsimd,))
         r_rows = rT.rearrange("(p i) t -> p i t", i=PACK)
         r_all = []
         for i in range(PACK):
             rows = keep.tile([P, T], F32, name="r_all%d" % i)
             nc.sync.dma_start(rows[:], r_rows[:, i, :])
             r_all.append(rows)
-        edge_w = keep.tile([P, J], F32, name="edge_w")
-        nc.sync.dma_start(edge_w[:], wgo)
 
         ident = keep.tile([P, P], F32, name="ident")
         make_identity(nc, ident[:])
         pages = []
-        for i in range(PACK):
-            page = keep.tile([P, T], F32, name="page%d" % i)
-            engine = nc.vector if i == 0 else nc.gpsimd
+
+        def clear_page(engine, tag):
+            page = keep.tile([P, T], F32, name="page%d" % len(pages), tag=tag)
             engine.memset(page[:], 0.0)
             pages.append(page)
 
-        picked_plane = keep.tile([P, 2, J], U8, name="picked_plane", align_bytes=64)
-        for side, lst in lists:
-            nc.vector.tensor_copy(picked_plane[:, side, :], tab_plane[:].indirect(lst[:]))
+        clear_page(nc.vector, "page0")
+        clear_page(nc.gpsimd, "page1")
 
-        def gather_words(words, h):
-            for side, lst in lists:
+        w_bank = psum.tile([P, P], F32, name="w_bank", tag="bank")
+        nc.tensor.transpose(w_bank[:], w_rows[:], ident[:])
+        edge_w = keep.tile([P, CHUNKS], F32, name="edge_w")
+        nc.scalar.copy(edge_w[:], w_bank[:, 0:CHUNKS])
+
+        def gather_plane(side, h, tag):
+            plane = keep.tile([P, HALF], U8, name="plane%d_%d" % (side, h), tag=tag, align_bytes=64)
+            nc.vector.tensor_copy(plane[:], tab_plane[:].indirect(entries(lists[side], h * HALF, HALF)))
+            picked_plane[side, h] = plane
+
+        def gather_words(h, tag):
+            words = keep.tile([P, 2, HALF], U32, name="words%d" % h, tag=tag, align_bytes=64)
+            for side in (SRC, TGT):
                 window = tab_codes[:].bitcast(U32)
-                nc.vector.tensor_copy(words[:, side, :], window.indirect(entries(lst, h * HALF, HALF)))
+                nc.vector.tensor_copy(words[:, side, :], window.indirect(entries(lists[side], h * HALF, HALF)))
+            picked_words.append(words)
 
-        words0 = keep.tile([P, 2, HALF], U32, name="words0", align_bytes=64)
-        gather_words(words0, 0)
+        picked_plane, picked_words = {}, []
+        gather_plane(SRC, 0, "plane_src0")
+        gather_plane(TGT, 0, "plane_tgt0")
+        gather_words(0, "words0")
+        gather_plane(SRC, 1, "plane_src1")
 
-        wb_bf = keep.tile([P, N, PACK], BF16, name="wb_bf", tag="wb_then_words", align_bytes=64)
-        for part, cols in zip(wb_raw, wb_cols):
-            nc.scalar.copy(
-                wb_bf[:, cols, :].rearrange("p (c e) i -> p c i e", e=4),
-                part[:].rearrange("p i (c e) -> p c i e", e=4),
-            )
         wb_codes = keep.tile([P, N], U32, name="wb_codes", align_bytes=64)
         wb_plane = keep.tile([P, N], U8, name="wb_plane", align_bytes=64)
-        nc.vector.quantize_mx(wb_codes[:].bitcast(FP8X4), wb_plane[:], wb_bf[:].rearrange("p n i -> p (n i)"))
+        for u, (part, cols) in enumerate(zip(wb_raw, wb_cols)):
+            wb_bf = keep.tile([P, N // 2, PACK], BF16, name="wb_bf%d" % u, tag="after_wb%d" % u, align_bytes=64)
+            nc.scalar.copy(
+                wb_bf[:].rearrange("p (c e) i -> p c i e", e=4),
+                part[:].rearrange("p i (c e) -> p c i e", e=4),
+            )
+            grouped = wb_bf[:].rearrange("p n i -> p (n i)")
+            nc.vector.quantize_mx(wb_codes[:, cols].bitcast(FP8X4), wb_plane[:, cols], grouped)
 
-        words1 = keep.tile([P, 2, HALF], U32, name="words1", tag="wb_then_words", align_bytes=64)
-        gather_words(words1, 1)
-        picked_words = [words0, words1]
+        gather_plane(TGT, 1, "after_wb0")
+        gather_words(1, "after_wb1")
 
         two_chunks = [
-            keep.tile([P, 2, PACK, P], F32, name="gated%d" % q, tag="gated_then_pairs%d" % q, align_bytes=64)
+            keep.tile([P, 2, PACK, P], F32, name="gated%d" % q, tag="gated_then_woven%d" % q, align_bytes=64)
             for q in range(CHUNKS // 2)
         ]
         gated = [two_chunks[c // 2][:, c % 2, :, :] for c in range(CHUNKS)]
 
         def gate(c):
-            words = picked_words[c // PER_HALF]
-            edges = slice(c * P, (c + 1) * P)
+            h = c // PER_HALF
+            words = picked_words[h]
             in_half = slice((c % PER_HALF) * P, (c % PER_HALF + 1) * P)
-            src_op = dict(lhsT=words[:, SRC, in_half].bitcast(FP8X4), lhsT_scale=picked_plane[:, SRC, edges])
-            tgt_op = dict(lhsT=words[:, TGT, in_half].bitcast(FP8X4), lhsT_scale=picked_plane[:, TGT, edges])
+            src_op = dict(lhsT=words[:, SRC, in_half].bitcast(FP8X4), lhsT_scale=picked_plane[SRC, h][:, in_half])
+            tgt_op = dict(lhsT=words[:, TGT, in_half].bitcast(FP8X4), lhsT_scale=picked_plane[TGT, h][:, in_half])
             wa_op = dict(rhs=wa_codes[:].bitcast(FP8X4), rhs_scale=w_planes[:, WA, :])
             wb_op = dict(rhs=wb_codes[:].bitcast(FP8X4), rhs_scale=wb_plane[:])
             wc_op = dict(rhs=wc_codes[:].bitcast(FP8X4), rhs_scale=w_planes[:, WC, :])
@@ -150,10 +170,14 @@ def tile_list_rgg_LP_kernel(
             nc.tensor.matmul_mx(ms[:], start=True, stop=True, **src_op, **wc_op)
             nc.tensor.matmul_mx(za[:], start=True, stop=False, **tgt_op, **wa_op)
             nc.tensor.matmul_mx(za[:], start=False, stop=True, **src_op, **wb_op)
-            eta = ring.tile([P, PACK, P], F32, name="eta")
+            if c == CHUNKS - 1:
+                eta = keep.tile([P, PACK, P], F32, name="last_eta", tag="page2")
+                msg = keep.tile([P, PACK, P], F32, name="last_msg", tag="page3")
+            else:
+                eta = ring.tile([P, PACK, P], F32, name="eta")
+                msg = ring.tile([P, PACK, P], F32, name="msg")
             nc.scalar.activation(eta[:], za[:].rearrange("j (m i) -> j i m", i=PACK), SIGMOID)
-            msg = ring.tile([P, PACK, P], F32, name="msg")
-            nc.scalar.copy(msg[:], ms[:].rearrange("j (m i) -> j i m", i=PACK))
+            nc.scalar.activation(msg[:], ms[:].rearrange("j (m i) -> j i m", i=PACK), COPY, scale=edge_w[:, c : c + 1])
             nc.gpsimd.tensor_tensor(gated[c], msg[:], eta[:], MULT)
 
         for c in range(CHUNKS - LATE_CHUNKS):
@@ -178,7 +202,9 @@ def tile_list_rgg_LP_kernel(
                 c = h * PER_HALF + b
                 nc.tensor.transpose(bank[:, b, :], r_picked[i][:, c * P : (c + 1) * P], ident[:])
             turned = keep.tile([P, PER_HALF, P], F32, name="r_by_edge%d_%d" % (i, h))
-            nc.scalar.copy(turned[:], bank[:])
+            for b in range(PER_HALF):
+                c = h * PER_HALF + b
+                nc.scalar.activation(turned[:, b, :], bank[:, b, :], COPY, scale=edge_w[:, c : c + 1])
             r_by_edge[i, h] = turned
 
         sums = [keep.tile([P, J], F32, name="sums%d" % i) for i in range(PACK)]
@@ -195,6 +221,8 @@ def tile_list_rgg_LP_kernel(
         add_and_turn_back(0, 0)
         for c in range(CHUNKS - LATE_CHUNKS, CHUNKS):
             gate(c)
+        clear_page(nc.gpsimd, "page2")
+        clear_page(nc.gpsimd, "page3")
         turn_r(1, 0, None)
         add_and_turn_back(1, 0)
         for i in range(EARLY_PAGES):
@@ -207,15 +235,14 @@ def tile_list_rgg_LP_kernel(
                 add_and_turn_back(i, h)
 
         out_rows = out_0.rearrange("(p i) t -> p i t", i=PACK)
-        pairs = [
-            keep.tile([P, 2, PIECE, 2], BF16, name="pairs%d" % q, tag="gated_then_pairs%d" % q, align_bytes=64)
+        woven = [
+            keep.tile([P, PIECE, PACK], BF16, name="woven%d" % q, tag="gated_then_woven%d" % q, align_bytes=64)
             for q in range(PIECES)
         ]
 
         def scatter(i, first, count):
-            edges = slice(first, first + count)
             places = pages[i][:].indirect(entries(tgt, first, count))
-            nc.vector.tensor_tensor(places, sums[i][:, edges], edge_w[:, edges], MULT)
+            nc.vector.tensor_copy(places, sums[i][:, first : first + count])
 
         for i in range(EARLY_PAGES):
             scatter(i, 0, HALF)
@@ -225,37 +252,41 @@ def tile_list_rgg_LP_kernel(
             else:
                 scatter(i, 0, J)
             nc.sync.dma_start(out_rows[:, i, :], pages[i][:])
+            if i == PACK - 1:
+                break
             for q in range(PIECES):
                 piece = pages[i][:, q * PIECE : (q + 1) * PIECE]
-                if i == PACK - 1 and q < VECTOR_PIECES:
-                    nc.vector.tensor_copy(pairs[q][:, i // 2, :, i % 2], piece)
-                elif i == PACK - 2 and q < VECTOR_PIECES:
-                    nc.scalar.copy(pairs[q][:, i // 2, :, :], piece.unsqueeze(2).to_broadcast([P, PIECE, 2]))
+                if q >= GPSIMD_PIECES:
+                    nc.scalar.copy(woven[q][:, :, i], piece)
+                elif i == PACK - 2:
+                    twice = piece.unsqueeze(2).to_broadcast([P, PIECE, 2])
+                    nc.gpsimd.tensor_scalar(woven[q][:, :, i:], twice, 1.0, 0.0, MULT, ADD)
                 else:
-                    nc.scalar.copy(pairs[q][:, i // 2, :, i % 2], piece)
-
-        last = (PIECES - 1) * PIECE
-        spans = [(q * PIECE, PIECE) for q in range(PIECES - 1)] + [(last, PIECE // 2), (last + PIECE // 2, PIECE // 2)]
-        woven = []
-        for first, width in spans:
-            q, inner = divmod(first, PIECE)
-            word = I32 if q < VECTOR_PIECES else U32
-            span = keep.tile([P, width * PACK], BF16, name="woven%d" % first, align_bytes=64)
-            dst = span[:].bitcast(word).rearrange("p (c u) -> p c u", u=2)
-            both = pairs[q][:].rearrange("p u c e -> p (u c e)").bitcast(word).rearrange("p (u c) -> p c u", u=2)
-            if q < VECTOR_PIECES:
-                nc.vector.tensor_copy(dst, both[:, inner : inner + width, :])
-            else:
-                nc.scalar.copy(dst, both[:, inner : inner + width, :])
-            woven.append(span)
+                    nc.gpsimd.tensor_scalar(woven[q][:, :, i], piece, 1.0, 0.0, MULT, ADD)
 
         out_plane = keep.tile([P, T], U8, name="out_plane", align_bytes=64)
         out_codes = keep.tile([P, T], I32, name="out_codes", align_bytes=64)
         out_words = words_of(out_1)
-        for (first, width), span in zip(spans, woven):
+        spans = []
+        for width in SPAN_WIDTHS:
+            first = sum(w for f, w in spans)
+            spans.append((first, width))
+        for first, width in spans:
+            q, inner = divmod(first, PIECE)
+            dst = woven[q][:, inner : inner + width, PACK - 1]
+            if first < VECTOR_COLUMNS:
+                nc.vector.tensor_copy(dst, pages[PACK - 1][:, first : first + width])
+            else:
+                nc.scalar.copy(dst, pages[PACK - 1][:, first : first + width])
+        stored = 0
+        for first, width in spans:
+            q, inner = divmod(first, PIECE)
             cols = slice(first, first + width)
-            nc.vector.quantize_mx(out_codes[:, cols].bitcast(FP8X4), out_plane[:, cols], span[:])
-            nc.sync.dma_start(out_words[:, cols], out_codes[:, cols])
+            span = woven[q][:, inner : inner + width, :].rearrange("p c i -> p (c i)")
+            nc.vector.quantize_mx(out_codes[:, cols].bitcast(FP8X4), out_plane[:, cols], span)
+            if cols.stop in STORE_ENDS:
+                nc.sync.dma_start(out_words[:, stored : cols.stop], out_codes[:, stored : cols.stop])
+                stored = cols.stop
         for quad in range(QUADRANTS):
             queue = nc.sync if quad % 2 == 0 else nc.scalar
             queue.dma_start(scale_rows(out_2, quad), live_rows(out_plane, quad))

@@ -32,7 +32,7 @@ PIECES = T // PIECE
 GPSIMD_PIECES = 2
 SPAN_WIDTHS = (512, 256, 256, 512, 256, 128, 128)
 VECTOR_COLUMNS = 768
-STORE_ENDS = (768, 1536, 2048)
+STORE_ENDS = (768, 1536, 1792, 2048)
 RING = 6
 SHARED_BANKS = 6
 SRC, TGT = 0, 1
@@ -105,13 +105,12 @@ def tile_list_rgg_LP_kernel(
         make_identity(nc, ident[:])
         pages = []
 
-        def clear_page(engine, tag):
+        def clear_page(tag):
             page = keep.tile([P, T], F32, name="page%d" % len(pages), tag=tag)
-            engine.memset(page[:], 0.0)
+            nc.gpsimd.memset(page[:], 0.0)
             pages.append(page)
 
-        clear_page(nc.vector, "page0")
-        clear_page(nc.gpsimd, "page1")
+        clear_page("page0")
 
         w_bank = psum.tile([P, P], F32, name="w_bank", tag="bank")
         nc.tensor.transpose(w_bank[:], w_rows[:], ident[:])
@@ -173,6 +172,9 @@ def tile_list_rgg_LP_kernel(
             if c == CHUNKS - 1:
                 eta = keep.tile([P, PACK, P], F32, name="last_eta", tag="page2")
                 msg = keep.tile([P, PACK, P], F32, name="last_msg", tag="page3")
+            elif c == CHUNKS - 2:
+                eta = keep.tile([P, PACK, P], F32, name="next_to_last_eta", tag="page1")
+                msg = ring.tile([P, PACK, P], F32, name="msg")
             else:
                 eta = ring.tile([P, PACK, P], F32, name="eta")
                 msg = ring.tile([P, PACK, P], F32, name="msg")
@@ -221,8 +223,8 @@ def tile_list_rgg_LP_kernel(
         add_and_turn_back(0, 0)
         for c in range(CHUNKS - LATE_CHUNKS, CHUNKS):
             gate(c)
-        clear_page(nc.gpsimd, "page2")
-        clear_page(nc.gpsimd, "page3")
+        for i in range(1, PACK):
+            clear_page("page%d" % i)
         turn_r(1, 0, None)
         add_and_turn_back(1, 0)
         for i in range(EARLY_PAGES):
@@ -264,7 +266,7 @@ def tile_list_rgg_LP_kernel(
                 else:
                     nc.gpsimd.tensor_scalar(woven[q][:, :, i], piece, 1.0, 0.0, MULT, ADD)
 
-        out_plane = keep.tile([P, T], U8, name="out_plane", align_bytes=64)
+        out_plane = keep.tile([P, PIECE], U8, name="out_plane", align_bytes=64)
         out_codes = keep.tile([P, T], I32, name="out_codes", align_bytes=64)
         out_words = words_of(out_1)
         spans = []
@@ -283,10 +285,11 @@ def tile_list_rgg_LP_kernel(
             q, inner = divmod(first, PIECE)
             cols = slice(first, first + width)
             span = woven[q][:, inner : inner + width, :].rearrange("p c i -> p (c i)")
-            nc.vector.quantize_mx(out_codes[:, cols].bitcast(FP8X4), out_plane[:, cols], span)
+            nc.vector.quantize_mx(out_codes[:, cols].bitcast(FP8X4), out_plane[4 * q :, inner : inner + width], span)
             if cols.stop in STORE_ENDS:
                 nc.sync.dma_start(out_words[:, stored : cols.stop], out_codes[:, stored : cols.stop])
                 stored = cols.stop
         for quad in range(QUADRANTS):
             queue = nc.sync if quad % 2 == 0 else nc.scalar
-            queue.dma_start(scale_rows(out_2, quad), live_rows(out_plane, quad))
+            rows = out_2[0, 4 * quad : 4 * quad + 4, :].bitcast(I32).rearrange("r (q c) -> q r c", q=PIECES)
+            queue.dma_start(rows, out_plane[32 * quad : 32 * quad + 16, :].bitcast(I32))

@@ -29,7 +29,7 @@ EARLY_PAGES = 2
 LATE_CHUNKS = 2
 PIECE = 512
 PIECES = T // PIECE
-GPSIMD_PIECES = 2
+GPSIMD_PIECES = 3
 SPAN_WIDTHS = (512, 256, 256, 512, 256, 128, 128)
 VECTOR_COLUMNS = 768
 STORE_ENDS = (768, 1536, 1792, 2048)
@@ -105,12 +105,13 @@ def tile_list_rgg_LP_kernel(
         make_identity(nc, ident[:])
         pages = []
 
-        def clear_page(tag):
+        def clear_page(engine, tag):
             page = keep.tile([P, T], F32, name="page%d" % len(pages), tag=tag)
-            nc.gpsimd.memset(page[:], 0.0)
+            engine.memset(page[:], 0.0)
             pages.append(page)
 
-        clear_page("page0")
+        clear_page(nc.vector, "page0")
+        clear_page(nc.gpsimd, "page1")
 
         w_bank = psum.tile([P, P], F32, name="w_bank", tag="bank")
         nc.tensor.transpose(w_bank[:], w_rows[:], ident[:])
@@ -172,9 +173,6 @@ def tile_list_rgg_LP_kernel(
             if c == CHUNKS - 1:
                 eta = keep.tile([P, PACK, P], F32, name="last_eta", tag="page2")
                 msg = keep.tile([P, PACK, P], F32, name="last_msg", tag="page3")
-            elif c == CHUNKS - 2:
-                eta = keep.tile([P, PACK, P], F32, name="next_to_last_eta", tag="page1")
-                msg = ring.tile([P, PACK, P], F32, name="msg")
             else:
                 eta = ring.tile([P, PACK, P], F32, name="eta")
                 msg = ring.tile([P, PACK, P], F32, name="msg")
@@ -223,8 +221,8 @@ def tile_list_rgg_LP_kernel(
         add_and_turn_back(0, 0)
         for c in range(CHUNKS - LATE_CHUNKS, CHUNKS):
             gate(c)
-        for i in range(1, PACK):
-            clear_page("page%d" % i)
+        clear_page(nc.gpsimd, "page2")
+        clear_page(nc.gpsimd, "page3")
         turn_r(1, 0, None)
         add_and_turn_back(1, 0)
         for i in range(EARLY_PAGES):
@@ -238,7 +236,13 @@ def tile_list_rgg_LP_kernel(
 
         out_rows = out_0.rearrange("(p i) t -> p i t", i=PACK)
         woven = [
-            keep.tile([P, PIECE, PACK], BF16, name="woven%d" % q, tag="gated_then_woven%d" % q, align_bytes=64)
+            keep.tile(
+                [P, PIECE, PACK],
+                BF16,
+                name="woven%d" % q,
+                tag="woven%d" % q if q < GPSIMD_PIECES else "gated_then_woven%d" % q,
+                align_bytes=64,
+            )
             for q in range(PIECES)
         ]
 

@@ -34,7 +34,8 @@ SPAN_WIDTHS = (512, 256, 256, 512, 256, 128, 128)
 VECTOR_COLUMNS = 768
 STORE_ENDS = (768, 1536, 1792, 2048)
 RING = 6
-SHARED_BANKS = 6
+MS_BANK = (0, 2, 4, 0, 2, 4, 6, 2)
+ZA_BANK = (1, 3, 5, 1, 3, 5, 7, 1)
 SRC, TGT = 0, 1
 WA, WC = 0, 1
 
@@ -46,7 +47,10 @@ def tile_list_rgg_LP_kernel(
     with ExitStack() as ctx:
         keep = ctx.enter_context(tc.tile_pool(name="keep", bufs=1))
         ring = ctx.enter_context(tc.tile_pool(name="ring", bufs=RING))
-        psum = ctx.enter_context(tc.psum_pool(name="psum", bufs=SHARED_BANKS))
+        psum = ctx.enter_context(tc.psum_pool(name="psum", bufs=1))
+
+        def bank_tile(bank, shape, name):
+            return psum.tile(shape, F32, name=name, tag="bank%d" % bank)
 
         def live_rows(plane, quad):
             return plane[32 * quad : 32 * quad + 4, :].bitcast(I32)
@@ -54,9 +58,9 @@ def tile_list_rgg_LP_kernel(
         def scale_rows(scales, quad):
             return scales[0, 4 * quad : 4 * quad + 4, :].bitcast(I32)
 
-        def load_plane(plane, scales, queues):
-            for quad in range(QUADRANTS):
-                queues[quad % len(queues)].dma_start(live_rows(plane, quad), scale_rows(scales, quad))
+        def load_plane(plane, scales, queue, quads):
+            for quad in quads:
+                queue.dma_start(live_rows(plane, quad), scale_rows(scales, quad))
 
         def words_of(packed):
             return packed[0].rearrange("p c i -> p (c i)").bitcast(I32)
@@ -75,8 +79,9 @@ def tile_list_rgg_LP_kernel(
         nc.gpsimd.memset(w_planes[:].rearrange("p w n -> p (w n)").bitcast(I32), 0)
         w_rows = keep.tile([P, P], F32, name="w_rows")
         nc.gpsimd.memset(w_rows[:], 0.0)
-        load_plane(tab_plane, tab_scales, (nc.scalar, nc.sync))
+        load_plane(tab_plane, tab_scales, nc.sync, range(QUADRANTS))
         nc.sync.dma_start(tgt[:], offs2)
+        load_plane(w_planes[:, WA, :], wa_scales, nc.sync, range(2))
         tab_codes = keep.tile([P, T], I32, name="tab_codes", align_bytes=64)
         nc.sync.dma_start(tab_codes[:], words_of(tab_words))
 
@@ -89,11 +94,11 @@ def tile_list_rgg_LP_kernel(
             wb_raw.append(part)
         wa_codes = keep.tile([P, N], I32, name="wa_codes", align_bytes=64)
         wc_codes = keep.tile([P, N], I32, name="wc_codes", align_bytes=64)
-        load_plane(w_planes[:, WC, :], wc_scales, (nc.sync,))
-        nc.sync.dma_start(w_rows[0:CHUNKS, :], wgo[0:1, :].rearrange("o (c j) -> (o c) j", j=P))
+        load_plane(w_planes[:, WC, :], wc_scales, nc.sync, range(QUADRANTS))
+        nc.gpsimd.dma_start(w_rows[0:CHUNKS, :], wgo[0:1, :].rearrange("o (c j) -> (o c) j", j=P))
         nc.sync.dma_start(wc_codes[:], words_of(wc_words))
         nc.sync.dma_start(wa_codes[:], words_of(wa_words))
-        load_plane(w_planes[:, WA, :], wa_scales, (nc.gpsimd,))
+        load_plane(w_planes[:, WA, :], wa_scales, nc.gpsimd, range(2, QUADRANTS))
         r_rows = rT.rearrange("(p i) t -> p i t", i=PACK)
         r_all = []
         for i in range(PACK):
@@ -112,16 +117,19 @@ def tile_list_rgg_LP_kernel(
 
         clear_page(nc.vector, "page0")
         clear_page(nc.gpsimd, "page1")
+        warm = keep.tile([P, 1], F32, name="warm")
+        nc.scalar.activation(warm[:], pages[0][:, 0:1], SIGMOID)
 
-        w_bank = psum.tile([P, P], F32, name="w_bank", tag="bank")
+        w_bank = bank_tile(6, [P, P], "w_bank")
         nc.tensor.transpose(w_bank[:], w_rows[:], ident[:])
         edge_w = keep.tile([P, CHUNKS], F32, name="edge_w")
         nc.scalar.copy(edge_w[:], w_bank[:, 0:CHUNKS])
 
-        def gather_plane(side, h, tag):
-            plane = keep.tile([P, HALF], U8, name="plane%d_%d" % (side, h), tag=tag, align_bytes=64)
-            nc.vector.tensor_copy(plane[:], tab_plane[:].indirect(entries(lists[side], h * HALF, HALF)))
-            picked_plane[side, h] = plane
+        picked_plane = keep.tile([P, 2, J], U8, name="picked_plane", align_bytes=64)
+        for side in (SRC, TGT):
+            nc.vector.tensor_copy(picked_plane[:, side, :], tab_plane[:].indirect(lists[side][:]))
+
+        picked_words = []
 
         def gather_words(h, tag):
             words = keep.tile([P, 2, HALF], U32, name="words%d" % h, tag=tag, align_bytes=64)
@@ -130,11 +138,7 @@ def tile_list_rgg_LP_kernel(
                 nc.vector.tensor_copy(words[:, side, :], window.indirect(entries(lists[side], h * HALF, HALF)))
             picked_words.append(words)
 
-        picked_plane, picked_words = {}, []
-        gather_plane(SRC, 0, "plane_src0")
-        gather_plane(TGT, 0, "plane_tgt0")
         gather_words(0, "words0")
-        gather_plane(SRC, 1, "plane_src1")
 
         wb_codes = keep.tile([P, N], U32, name="wb_codes", align_bytes=64)
         wb_plane = keep.tile([P, N], U8, name="wb_plane", align_bytes=64)
@@ -147,7 +151,6 @@ def tile_list_rgg_LP_kernel(
             grouped = wb_bf[:].rearrange("p n i -> p (n i)")
             nc.vector.quantize_mx(wb_codes[:, cols].bitcast(FP8X4), wb_plane[:, cols], grouped)
 
-        gather_plane(TGT, 1, "after_wb0")
         gather_words(1, "after_wb1")
 
         two_chunks = [
@@ -158,15 +161,15 @@ def tile_list_rgg_LP_kernel(
 
         def gate(c):
             h = c // PER_HALF
-            words = picked_words[h]
+            edges = slice(c * P, (c + 1) * P)
             in_half = slice((c % PER_HALF) * P, (c % PER_HALF + 1) * P)
-            src_op = dict(lhsT=words[:, SRC, in_half].bitcast(FP8X4), lhsT_scale=picked_plane[SRC, h][:, in_half])
-            tgt_op = dict(lhsT=words[:, TGT, in_half].bitcast(FP8X4), lhsT_scale=picked_plane[TGT, h][:, in_half])
+            src_op = dict(lhsT=picked_words[h][:, SRC, in_half].bitcast(FP8X4), lhsT_scale=picked_plane[:, SRC, edges])
+            tgt_op = dict(lhsT=picked_words[h][:, TGT, in_half].bitcast(FP8X4), lhsT_scale=picked_plane[:, TGT, edges])
             wa_op = dict(rhs=wa_codes[:].bitcast(FP8X4), rhs_scale=w_planes[:, WA, :])
             wb_op = dict(rhs=wb_codes[:].bitcast(FP8X4), rhs_scale=wb_plane[:])
             wc_op = dict(rhs=wc_codes[:].bitcast(FP8X4), rhs_scale=w_planes[:, WC, :])
-            ms = psum.tile([P, N], F32, name="ms", tag="bank")
-            za = psum.tile([P, N], F32, name="za", tag="bank")
+            ms = bank_tile(MS_BANK[c], [P, N], "ms")
+            za = bank_tile(ZA_BANK[c], [P, N], "za")
             nc.tensor.matmul_mx(ms[:], start=True, stop=True, **src_op, **wc_op)
             nc.tensor.matmul_mx(za[:], start=True, stop=False, **tgt_op, **wa_op)
             nc.tensor.matmul_mx(za[:], start=False, stop=True, **src_op, **wb_op)
@@ -189,15 +192,10 @@ def tile_list_rgg_LP_kernel(
             nc.vector.tensor_copy(rows[:], r_all[i][:].indirect(tgt[:]))
             r_picked.append(rows)
 
-        def transposed_bank(first_sum_bank):
-            if first_sum_bank is None:
-                return psum.tile([P, PER_HALF, P], F32, name="turned", tag="bank")
-            return psum.tile([P, PER_HALF, P], F32, name="turned", tag="first_sum%d" % first_sum_bank, bufs=1)
-
         r_by_edge = {}
 
-        def turn_r(i, h, first_sum_bank):
-            bank = transposed_bank(first_sum_bank)
+        def turn_r(i, h, where):
+            bank = bank_tile(where, [P, PER_HALF, P], "turned")
             for b in range(PER_HALF):
                 c = h * PER_HALF + b
                 nc.tensor.transpose(bank[:, b, :], r_picked[i][:, c * P : (c + 1) * P], ident[:])
@@ -209,30 +207,34 @@ def tile_list_rgg_LP_kernel(
 
         sums = [keep.tile([P, J], F32, name="sums%d" % i) for i in range(PACK)]
 
-        def add_and_turn_back(i, h):
-            bank = transposed_bank(i if h == 0 and i < EARLY_PAGES else None)
+        def add_and_turn_back(i, h, where):
+            bank = bank_tile(where, [P, PER_HALF, P], "summed")
             for b in range(PER_HALF):
                 terms = (r_by_edge[i, h][:, b, :], gated[h * PER_HALF + b][:, i, :])
                 for term, first in zip(terms, (True, False)):
                     nc.tensor.matmul(bank[:, b, :], term, ident[:], start=first, stop=not first, is_transpose=True)
             nc.scalar.copy(sums[i][:, h * HALF : (h + 1) * HALF], bank[:].rearrange("p b j -> p (b j)"))
 
-        turn_r(0, 0, 1)
-        add_and_turn_back(0, 0)
+        turn_r(0, 0, 0)
+        add_and_turn_back(0, 0, 2)
         for c in range(CHUNKS - LATE_CHUNKS, CHUNKS):
             gate(c)
         clear_page(nc.gpsimd, "page2")
         clear_page(nc.gpsimd, "page3")
-        turn_r(1, 0, None)
-        add_and_turn_back(1, 0)
-        for i in range(EARLY_PAGES):
-            turn_r(i, 1, None)
-            add_and_turn_back(i, 1)
-        for i in range(EARLY_PAGES, PACK):
-            for h in range(2):
-                turn_r(i, h, h)
-            for h in range(2):
-                add_and_turn_back(i, h)
+        turn_r(1, 0, 6)
+        turn_r(0, 1, 5)
+        add_and_turn_back(1, 0, 3)
+        turn_r(1, 1, 7)
+        add_and_turn_back(0, 1, 6)
+        turn_r(2, 0, 2)
+        add_and_turn_back(1, 1, 1)
+        turn_r(2, 1, 3)
+        add_and_turn_back(2, 0, 4)
+        turn_r(3, 0, 6)
+        add_and_turn_back(2, 1, 0)
+        turn_r(3, 1, 1)
+        add_and_turn_back(3, 0, 5)
+        add_and_turn_back(3, 1, 7)
 
         out_rows = out_0.rearrange("(p i) t -> p i t", i=PACK)
         woven = [

@@ -117,13 +117,13 @@ def tile_list_rgg_LP_kernel(
 
         clear_page(nc.vector, "page0")
         clear_page(nc.gpsimd, "page1")
-        warm = keep.tile([P, 1], F32, name="warm")
-        nc.scalar.activation(warm[:], pages[0][:, 0:1], SIGMOID)
 
-        w_bank = bank_tile(6, [P, P], "w_bank")
-        nc.tensor.transpose(w_bank[:], w_rows[:], ident[:])
         edge_w = keep.tile([P, CHUNKS], F32, name="edge_w")
-        nc.scalar.copy(edge_w[:], w_bank[:, 0:CHUNKS])
+
+        def spread_weights(where):
+            w_bank = bank_tile(where, [P, P], "w_bank")
+            nc.tensor.transpose(w_bank[:], w_rows[:], ident[:])
+            nc.scalar.copy(edge_w[:], w_bank[:, 0:CHUNKS])
 
         picked_plane = keep.tile([P, 2, J], U8, name="picked_plane", align_bytes=64)
         for side in (SRC, TGT):
@@ -180,6 +180,8 @@ def tile_list_rgg_LP_kernel(
                 eta = ring.tile([P, PACK, P], F32, name="eta")
                 msg = ring.tile([P, PACK, P], F32, name="msg")
             nc.scalar.activation(eta[:], za[:].rearrange("j (m i) -> j i m", i=PACK), SIGMOID)
+            if c == 0:
+                spread_weights(ZA_BANK[c])
             nc.scalar.activation(msg[:], ms[:].rearrange("j (m i) -> j i m", i=PACK), COPY, scale=edge_w[:, c : c + 1])
             nc.gpsimd.tensor_tensor(gated[c], msg[:], eta[:], MULT)
 

@@ -32,10 +32,10 @@ PIECES = T // PIECE
 GPSIMD_PIECES = 3
 SPAN_WIDTHS = (512, 256, 256, 512, 256, 128, 128)
 VECTOR_COLUMNS = 768
-STORE_ENDS = (768, 1536, 1792, 2048)
+STORE_ENDS = (1024, 1792, 2048)
 RING = 6
-MS_BANK = (0, 2, 4, 0, 2, 4, 6, 2)
-ZA_BANK = (1, 3, 5, 1, 3, 5, 7, 1)
+CHUNKS_IN_PSUM = 3
+SYNC_WA_QUADRANTS = 2
 SRC, TGT = 0, 1
 WA, WC = 0, 1
 
@@ -49,8 +49,16 @@ def tile_list_rgg_LP_kernel(
         ring = ctx.enter_context(tc.tile_pool(name="ring", bufs=RING))
         psum = ctx.enter_context(tc.psum_pool(name="psum", bufs=1))
 
-        def bank_tile(bank, shape, name):
-            return psum.tile(shape, F32, name=name, tag="bank%d" % bank)
+        bank_of = {}
+        opened = []
+
+        def take_bank(user, after, shape):
+            if after is None:
+                bank_of[user] = len(opened)
+                opened.append(user)
+            else:
+                bank_of[user] = bank_of[after]
+            return psum.tile(shape, F32, name=user[0], tag="bank%d" % bank_of[user])
 
         def live_rows(plane, quad):
             return plane[32 * quad : 32 * quad + 4, :].bitcast(I32)
@@ -81,9 +89,9 @@ def tile_list_rgg_LP_kernel(
         nc.gpsimd.memset(w_rows[:], 0.0)
         load_plane(tab_plane, tab_scales, nc.sync, range(QUADRANTS))
         nc.sync.dma_start(tgt[:], offs2)
-        load_plane(w_planes[:, WA, :], wa_scales, nc.sync, range(2))
         tab_codes = keep.tile([P, T], I32, name="tab_codes", align_bytes=64)
         nc.sync.dma_start(tab_codes[:], words_of(tab_words))
+        load_plane(w_planes[:, WA, :], wa_scales, nc.sync, range(SYNC_WA_QUADRANTS))
 
         wb_rows = wb.rearrange("(p i) n -> p i n", i=PACK)
         wb_cols = [slice(0, N // 2), slice(N // 2, N)]
@@ -98,7 +106,7 @@ def tile_list_rgg_LP_kernel(
         nc.gpsimd.dma_start(w_rows[0:CHUNKS, :], wgo[0:1, :].rearrange("o (c j) -> (o c) j", j=P))
         nc.sync.dma_start(wc_codes[:], words_of(wc_words))
         nc.sync.dma_start(wa_codes[:], words_of(wa_words))
-        load_plane(w_planes[:, WA, :], wa_scales, nc.gpsimd, range(2, QUADRANTS))
+        load_plane(w_planes[:, WA, :], wa_scales, nc.gpsimd, range(SYNC_WA_QUADRANTS, QUADRANTS))
         r_rows = rT.rearrange("(p i) t -> p i t", i=PACK)
         r_all = []
         for i in range(PACK):
@@ -108,20 +116,21 @@ def tile_list_rgg_LP_kernel(
 
         ident = keep.tile([P, P], F32, name="ident")
         make_identity(nc, ident[:])
+
         pages = []
 
-        def clear_page(engine, tag):
-            page = keep.tile([P, T], F32, name="page%d" % len(pages), tag=tag)
+        def clear_page(engine):
+            page = keep.tile([P, T], F32, name="page%d" % len(pages), tag="page%d" % len(pages))
             engine.memset(page[:], 0.0)
             pages.append(page)
 
-        clear_page(nc.vector, "page0")
-        clear_page(nc.gpsimd, "page1")
+        clear_page(nc.vector)
+        clear_page(nc.gpsimd)
 
         edge_w = keep.tile([P, CHUNKS], F32, name="edge_w")
 
-        def spread_weights(where):
-            w_bank = bank_tile(where, [P, P], "w_bank")
+        def turn_weights(after):
+            w_bank = take_bank(("weights",), after, [P, P])
             nc.tensor.transpose(w_bank[:], w_rows[:], ident[:])
             nc.scalar.copy(edge_w[:], w_bank[:, 0:CHUNKS])
 
@@ -159,7 +168,7 @@ def tile_list_rgg_LP_kernel(
         ]
         gated = [two_chunks[c // 2][:, c % 2, :, :] for c in range(CHUNKS)]
 
-        def gate(c):
+        def gate(c, ms_after, za_after):
             h = c // PER_HALF
             edges = slice(c * P, (c + 1) * P)
             in_half = slice((c % PER_HALF) * P, (c % PER_HALF + 1) * P)
@@ -168,8 +177,8 @@ def tile_list_rgg_LP_kernel(
             wa_op = dict(rhs=wa_codes[:].bitcast(FP8X4), rhs_scale=w_planes[:, WA, :])
             wb_op = dict(rhs=wb_codes[:].bitcast(FP8X4), rhs_scale=wb_plane[:])
             wc_op = dict(rhs=wc_codes[:].bitcast(FP8X4), rhs_scale=w_planes[:, WC, :])
-            ms = bank_tile(MS_BANK[c], [P, N], "ms")
-            za = bank_tile(ZA_BANK[c], [P, N], "za")
+            ms = take_bank(("ms", c), ms_after, [P, N])
+            za = take_bank(("za", c), za_after, [P, N])
             nc.tensor.matmul_mx(ms[:], start=True, stop=True, **src_op, **wc_op)
             nc.tensor.matmul_mx(za[:], start=True, stop=False, **tgt_op, **wa_op)
             nc.tensor.matmul_mx(za[:], start=False, stop=True, **src_op, **wb_op)
@@ -181,12 +190,15 @@ def tile_list_rgg_LP_kernel(
                 msg = ring.tile([P, PACK, P], F32, name="msg")
             nc.scalar.activation(eta[:], za[:].rearrange("j (m i) -> j i m", i=PACK), SIGMOID)
             if c == 0:
-                spread_weights(ZA_BANK[c])
+                turn_weights(("za", c))
             nc.scalar.activation(msg[:], ms[:].rearrange("j (m i) -> j i m", i=PACK), COPY, scale=edge_w[:, c : c + 1])
             nc.gpsimd.tensor_tensor(gated[c], msg[:], eta[:], MULT)
 
-        for c in range(CHUNKS - LATE_CHUNKS):
-            gate(c)
+        for c in range(CHUNKS_IN_PSUM):
+            gate(c, None, None)
+        gate(CHUNKS_IN_PSUM, ("ms", 0), ("weights",))
+        for c in range(CHUNKS_IN_PSUM + 1, CHUNKS - LATE_CHUNKS):
+            gate(c, ("ms", c - CHUNKS_IN_PSUM), ("za", c - CHUNKS_IN_PSUM))
 
         r_picked = []
         for i in range(PACK):
@@ -196,8 +208,8 @@ def tile_list_rgg_LP_kernel(
 
         r_by_edge = {}
 
-        def turn_r(i, h, where):
-            bank = bank_tile(where, [P, PER_HALF, P], "turned")
+        def turn_r(i, h, after):
+            bank = take_bank(("turned", i, h), after, [P, PER_HALF, P])
             for b in range(PER_HALF):
                 c = h * PER_HALF + b
                 nc.tensor.transpose(bank[:, b, :], r_picked[i][:, c * P : (c + 1) * P], ident[:])
@@ -209,34 +221,34 @@ def tile_list_rgg_LP_kernel(
 
         sums = [keep.tile([P, J], F32, name="sums%d" % i) for i in range(PACK)]
 
-        def add_and_turn_back(i, h, where):
-            bank = bank_tile(where, [P, PER_HALF, P], "summed")
+        def add_and_turn_back(i, h, after):
+            bank = take_bank(("summed", i, h), after, [P, PER_HALF, P])
             for b in range(PER_HALF):
                 terms = (r_by_edge[i, h][:, b, :], gated[h * PER_HALF + b][:, i, :])
                 for term, first in zip(terms, (True, False)):
                     nc.tensor.matmul(bank[:, b, :], term, ident[:], start=first, stop=not first, is_transpose=True)
             nc.scalar.copy(sums[i][:, h * HALF : (h + 1) * HALF], bank[:].rearrange("p b j -> p (b j)"))
 
-        turn_r(0, 0, 0)
-        add_and_turn_back(0, 0, 2)
-        for c in range(CHUNKS - LATE_CHUNKS, CHUNKS):
-            gate(c)
-        clear_page(nc.gpsimd, "page2")
-        clear_page(nc.gpsimd, "page3")
-        turn_r(1, 0, 6)
-        turn_r(0, 1, 5)
-        add_and_turn_back(1, 0, 3)
-        turn_r(1, 1, 7)
-        add_and_turn_back(0, 1, 6)
-        turn_r(2, 0, 2)
-        add_and_turn_back(1, 1, 1)
-        turn_r(2, 1, 3)
-        add_and_turn_back(2, 0, 4)
-        turn_r(3, 0, 6)
-        add_and_turn_back(2, 1, 0)
-        turn_r(3, 1, 1)
-        add_and_turn_back(3, 0, 5)
-        add_and_turn_back(3, 1, 7)
+        turn_r(0, 0, ("ms", 3))
+        add_and_turn_back(0, 0, ("ms", 4))
+        gate(CHUNKS - 2, None, None)
+        gate(CHUNKS - 1, ("summed", 0, 0), ("za", 3))
+        for i in range(EARLY_PAGES, PACK):
+            clear_page(nc.gpsimd)
+        turn_r(1, 0, ("ms", 6))
+        turn_r(0, 1, ("za", 5))
+        add_and_turn_back(1, 0, ("za", 4))
+        turn_r(1, 1, ("za", 6))
+        add_and_turn_back(0, 1, ("turned", 1, 0))
+        turn_r(2, 0, ("ms", 7))
+        add_and_turn_back(1, 1, ("za", 7))
+        turn_r(2, 1, ("summed", 1, 0))
+        add_and_turn_back(2, 0, ("ms", 5))
+        turn_r(3, 0, ("summed", 0, 1))
+        add_and_turn_back(2, 1, ("turned", 0, 0))
+        turn_r(3, 1, ("summed", 1, 1))
+        add_and_turn_back(3, 0, ("turned", 0, 1))
+        add_and_turn_back(3, 1, ("turned", 1, 1))
 
         out_rows = out_0.rearrange("(p i) t -> p i t", i=PACK)
         woven = [
@@ -277,10 +289,7 @@ def tile_list_rgg_LP_kernel(
         out_plane = keep.tile([P, PIECE], U8, name="out_plane", align_bytes=64)
         out_codes = keep.tile([P, T], I32, name="out_codes", align_bytes=64)
         out_words = words_of(out_1)
-        spans = []
-        for width in SPAN_WIDTHS:
-            first = sum(w for f, w in spans)
-            spans.append((first, width))
+        spans = [(sum(SPAN_WIDTHS[:s]), width) for s, width in enumerate(SPAN_WIDTHS)]
         for first, width in spans:
             q, inner = divmod(first, PIECE)
             dst = woven[q][:, inner : inner + width, PACK - 1]

@@ -31,8 +31,8 @@ PIECE = 512
 PIECES = T // PIECE
 GPSIMD_PIECES = 3
 SPAN_WIDTHS = (512, 256, 256, 512, 256, 128, 128)
-VECTOR_COLUMNS = 768
-STORE_ENDS = (1024, 1792, 2048)
+VECTOR_COLUMNS = 832
+STORE_ENDS = (768, 1536, 2048)
 RING = 6
 CHUNKS_IN_PSUM = 3
 SYNC_WA_QUADRANTS = 2
@@ -60,15 +60,14 @@ def tile_list_rgg_LP_kernel(
                 bank_of[user] = bank_of[after]
             return psum.tile(shape, F32, name=user[0], tag="bank%d" % bank_of[user])
 
-        def live_rows(plane, quad):
-            return plane[32 * quad : 32 * quad + 4, :].bitcast(I32)
+        def load_plane(plane, scales, queue, rows):
+            for r in rows:
+                queue.dma_start(plane[r:P:32, :].bitcast(I32), scales[0, r : 4 * QUADRANTS : 4, :].bitcast(I32))
 
-        def scale_rows(scales, quad):
-            return scales[0, 4 * quad : 4 * quad + 4, :].bitcast(I32)
-
-        def load_plane(plane, scales, queue, quads):
+        def load_quadrants(plane, scales, queue, quads):
             for quad in quads:
-                queue.dma_start(live_rows(plane, quad), scale_rows(scales, quad))
+                rows = scales[0, 4 * quad : 4 * quad + 4, :].bitcast(I32)
+                queue.dma_start(plane[32 * quad : 32 * quad + 4, :].bitcast(I32), rows)
 
         def words_of(packed):
             return packed[0].rearrange("p c i -> p (c i)").bitcast(I32)
@@ -79,6 +78,7 @@ def tile_list_rgg_LP_kernel(
         src = keep.tile([P, J // LIST_ROWS], U16, name="src")
         tgt = keep.tile([P, J // LIST_ROWS], U16, name="tgt")
         nc.sync.dma_start(src[:], offs)
+        nc.sync.dma_start(tgt[:], offs2)
         lists = (src, tgt)
 
         tab_plane = keep.tile([P, T], U8, name="tab_plane", align_bytes=64)
@@ -88,25 +88,24 @@ def tile_list_rgg_LP_kernel(
         w_rows = keep.tile([P, P], F32, name="w_rows")
         nc.gpsimd.memset(w_rows[:], 0.0)
         load_plane(tab_plane, tab_scales, nc.sync, range(QUADRANTS))
-        nc.sync.dma_start(tgt[:], offs2)
         tab_codes = keep.tile([P, T], I32, name="tab_codes", align_bytes=64)
         nc.sync.dma_start(tab_codes[:], words_of(tab_words))
-        load_plane(w_planes[:, WA, :], wa_scales, nc.sync, range(SYNC_WA_QUADRANTS))
+        load_quadrants(w_planes[:, WA, :], wa_scales, nc.sync, range(SYNC_WA_QUADRANTS))
 
         wb_rows = wb.rearrange("(p i) n -> p i n", i=PACK)
         wb_cols = [slice(0, N // 2), slice(N // 2, N)]
         wb_raw = []
         for u, cols in enumerate(wb_cols):
-            part = keep.tile([P, PACK, N // 2], F32, name="wb_raw%d" % u)
+            part = keep.tile([P, PACK, N // 2], F32, name="wb_raw%d" % u, tag="wb_raw%d" % u, align_bytes=64)
             nc.sync.dma_start(part[:], wb_rows[:, :, cols])
             wb_raw.append(part)
         wa_codes = keep.tile([P, N], I32, name="wa_codes", align_bytes=64)
         wc_codes = keep.tile([P, N], I32, name="wc_codes", align_bytes=64)
-        load_plane(w_planes[:, WC, :], wc_scales, nc.sync, range(QUADRANTS))
+        load_quadrants(w_planes[:, WC, :], wc_scales, nc.sync, range(QUADRANTS))
         nc.gpsimd.dma_start(w_rows[0:CHUNKS, :], wgo[0:1, :].rearrange("o (c j) -> (o c) j", j=P))
         nc.sync.dma_start(wc_codes[:], words_of(wc_words))
         nc.sync.dma_start(wa_codes[:], words_of(wa_words))
-        load_plane(w_planes[:, WA, :], wa_scales, nc.gpsimd, range(SYNC_WA_QUADRANTS, QUADRANTS))
+        load_quadrants(w_planes[:, WA, :], wa_scales, nc.gpsimd, range(SYNC_WA_QUADRANTS, QUADRANTS))
         r_rows = rT.rearrange("(p i) t -> p i t", i=PACK)
         r_all = []
         for i in range(PACK):
@@ -152,7 +151,7 @@ def tile_list_rgg_LP_kernel(
         wb_codes = keep.tile([P, N], U32, name="wb_codes", align_bytes=64)
         wb_plane = keep.tile([P, N], U8, name="wb_plane", align_bytes=64)
         for u, (part, cols) in enumerate(zip(wb_raw, wb_cols)):
-            wb_bf = keep.tile([P, N // 2, PACK], BF16, name="wb_bf%d" % u, tag="after_wb%d" % u, align_bytes=64)
+            wb_bf = keep.tile([P, N // 2, PACK], BF16, name="wb_bf%d" % u, align_bytes=64)
             nc.scalar.copy(
                 wb_bf[:].rearrange("p (c e) i -> p c i e", e=4),
                 part[:].rearrange("p i (c e) -> p c i e", e=4),
@@ -160,7 +159,7 @@ def tile_list_rgg_LP_kernel(
             grouped = wb_bf[:].rearrange("p n i -> p (n i)")
             nc.vector.quantize_mx(wb_codes[:, cols].bitcast(FP8X4), wb_plane[:, cols], grouped)
 
-        gather_words(1, "after_wb1")
+        gather_words(1, "wb_raw1")
 
         two_chunks = [
             keep.tile([P, 2, PACK, P], F32, name="gated%d" % q, tag="gated_then_woven%d" % q, align_bytes=64)
@@ -229,10 +228,10 @@ def tile_list_rgg_LP_kernel(
                     nc.tensor.matmul(bank[:, b, :], term, ident[:], start=first, stop=not first, is_transpose=True)
             nc.scalar.copy(sums[i][:, h * HALF : (h + 1) * HALF], bank[:].rearrange("p b j -> p (b j)"))
 
-        turn_r(0, 0, ("ms", 3))
-        add_and_turn_back(0, 0, ("ms", 4))
+        turn_r(0, 0, ("za", 3))
+        add_and_turn_back(0, 0, ("ms", 3))
         gate(CHUNKS - 2, None, None)
-        gate(CHUNKS - 1, ("summed", 0, 0), ("za", 3))
+        gate(CHUNKS - 1, ("summed", 0, 0), ("ms", 4))
         for i in range(EARLY_PAGES, PACK):
             clear_page(nc.gpsimd)
         turn_r(1, 0, ("ms", 6))
@@ -290,13 +289,14 @@ def tile_list_rgg_LP_kernel(
         out_codes = keep.tile([P, T], I32, name="out_codes", align_bytes=64)
         out_words = words_of(out_1)
         spans = [(sum(SPAN_WIDTHS[:s]), width) for s, width in enumerate(SPAN_WIDTHS)]
-        for first, width in spans:
+        cuts = sorted(set([first for first, width in spans] + [VECTOR_COLUMNS, T]))
+        for first, end in zip(cuts, cuts[1:]):
             q, inner = divmod(first, PIECE)
-            dst = woven[q][:, inner : inner + width, PACK - 1]
+            dst = woven[q][:, inner : inner + end - first, PACK - 1]
             if first < VECTOR_COLUMNS:
-                nc.vector.tensor_copy(dst, pages[PACK - 1][:, first : first + width])
+                nc.vector.tensor_copy(dst, pages[PACK - 1][:, first:end])
             else:
-                nc.scalar.copy(dst, pages[PACK - 1][:, first : first + width])
+                nc.scalar.copy(dst, pages[PACK - 1][:, first:end])
         stored = 0
         for first, width in spans:
             q, inner = divmod(first, PIECE)

@@ -36,6 +36,9 @@ STORE_ENDS = (768, 1536, 2048)
 RING = 6
 CHUNKS_IN_PSUM = 3
 SYNC_WA_QUADRANTS = 2
+QUARTER = J // 4
+PLACES = (0, 1024, 1536, 6144, 2048, 6656, 2560, 7168, 3072, 7680, 10240, 12288)
+HELD = 14336
 SRC, TGT = 0, 1
 WA, WC = 0, 1
 
@@ -47,6 +50,7 @@ def tile_list_rgg_LP_kernel(
     with ExitStack() as ctx:
         keep = ctx.enter_context(tc.tile_pool(name="keep", bufs=1))
         ring = ctx.enter_context(tc.tile_pool(name="ring", bufs=RING))
+        placed = ctx.enter_context(tc.tile_pool(name="placed", bufs=1))
         psum = ctx.enter_context(tc.psum_pool(name="psum", bufs=1))
 
         bank_of = {}
@@ -107,24 +111,23 @@ def tile_list_rgg_LP_kernel(
         nc.sync.dma_start(wa_codes[:], words_of(wa_words))
         load_quadrants(w_planes[:, WA, :], wa_scales, nc.gpsimd, range(SYNC_WA_QUADRANTS, QUADRANTS))
         r_rows = rT.rearrange("(p i) t -> p i t", i=PACK)
-        r_all = []
-        for i in range(PACK):
-            rows = keep.tile([P, T], F32, name="r_all%d" % i)
-            nc.sync.dma_start(rows[:], r_rows[:, i, :])
-            r_all.append(rows)
+        r_all = [keep.tile([P, T], F32, name="r_all%d" % i) for i in range(PACK)]
+        for i in (0, 2, 1, 3):
+            nc.sync.dma_start(r_all[i][:], r_rows[:, i, :])
 
         ident = keep.tile([P, P], F32, name="ident")
         make_identity(nc, ident[:])
 
         pages = []
 
-        def clear_page(engine):
-            page = keep.tile([P, T], F32, name="page%d" % len(pages), tag="page%d" % len(pages))
+        def clear_page(engine, tag):
+            page = keep.tile([P, T], F32, name="page%d" % len(pages), tag=tag, align_bytes=64)
             engine.memset(page[:], 0.0)
             pages.append(page)
 
-        clear_page(nc.vector)
-        clear_page(nc.gpsimd)
+        clear_page(nc.vector, "page0")
+        clear_page(nc.gpsimd, "page1")
+        clear_page(nc.gpsimd, "page2")
 
         edge_w = keep.tile([P, CHUNKS], F32, name="edge_w")
 
@@ -151,7 +154,7 @@ def tile_list_rgg_LP_kernel(
         wb_codes = keep.tile([P, N], U32, name="wb_codes", align_bytes=64)
         wb_plane = keep.tile([P, N], U8, name="wb_plane", align_bytes=64)
         for u, (part, cols) in enumerate(zip(wb_raw, wb_cols)):
-            wb_bf = keep.tile([P, N // 2, PACK], BF16, name="wb_bf%d" % u, align_bytes=64)
+            wb_bf = keep.tile([P, N // 2, PACK], BF16, name="wb_bf%d" % u, tag="wb_bf%d" % u, align_bytes=64)
             nc.scalar.copy(
                 wb_bf[:].rearrange("p (c e) i -> p c i e", e=4),
                 part[:].rearrange("p i (c e) -> p c i e", e=4),
@@ -160,6 +163,7 @@ def tile_list_rgg_LP_kernel(
             nc.vector.quantize_mx(wb_codes[:, cols].bitcast(FP8X4), wb_plane[:, cols], grouped)
 
         gather_words(1, "wb_raw1")
+        clear_page(nc.gpsimd, "wb_bf1")
 
         two_chunks = [
             keep.tile([P, 2, PACK, P], F32, name="gated%d" % q, tag="gated_then_woven%d" % q, align_bytes=64)
@@ -181,9 +185,9 @@ def tile_list_rgg_LP_kernel(
             nc.tensor.matmul_mx(ms[:], start=True, stop=True, **src_op, **wc_op)
             nc.tensor.matmul_mx(za[:], start=True, stop=False, **tgt_op, **wa_op)
             nc.tensor.matmul_mx(za[:], start=False, stop=True, **src_op, **wb_op)
-            if c == CHUNKS - 1:
-                eta = keep.tile([P, PACK, P], F32, name="last_eta", tag="page2")
-                msg = keep.tile([P, PACK, P], F32, name="last_msg", tag="page3")
+            if c == PER_HALF:
+                eta = placed.tile([P, PACK, P], F32, name="held_eta", offset=HELD + 1024)
+                msg = ring.tile([P, PACK, P], F32, name="msg")
             else:
                 eta = ring.tile([P, PACK, P], F32, name="eta")
                 msg = ring.tile([P, PACK, P], F32, name="msg")
@@ -196,58 +200,102 @@ def tile_list_rgg_LP_kernel(
         for c in range(CHUNKS_IN_PSUM):
             gate(c, None, None)
         gate(CHUNKS_IN_PSUM, ("ms", 0), ("weights",))
-        for c in range(CHUNKS_IN_PSUM + 1, CHUNKS - LATE_CHUNKS):
-            gate(c, ("ms", c - CHUNKS_IN_PSUM), ("za", c - CHUNKS_IN_PSUM))
 
-        r_picked = []
-        for i in range(PACK):
-            rows = keep.tile([P, J], F32, name="r_picked%d" % i)
-            nc.vector.tensor_copy(rows[:], r_all[i][:].indirect(tgt[:]))
-            r_picked.append(rows)
+        picked = {}
 
+        def gather_r(i, first, count, rows):
+            nc.vector.tensor_copy(rows[:], r_all[i][:].indirect(entries(tgt, first, count)))
+            for b in range(count // P):
+                picked[i, first // P + b] = rows[:, b * P : (b + 1) * P]
+
+        gather_r(0, 0, J, keep.tile([P, J], F32, name="picked0"))
+        gather_r(2, 0, J, keep.tile([P, J], F32, name="picked2"))
+        gather_r(1, 0, QUARTER, placed.tile([P, QUARTER], F32, name="picked1_first", offset=HELD + 512))
+        gather_r(1, QUARTER, J - QUARTER, keep.tile([P, J - QUARTER], F32, name="picked1_rest"))
+
+        runs = [(i, first, QUARTER) for first in range(0, J, QUARTER) for i in range(EARLY_PAGES)]
+        runs += [(i, first, HALF) for i in range(EARLY_PAGES, PACK) for first in range(0, J, HALF)]
         r_by_edge = {}
 
-        def turn_r(i, h, after):
-            bank = take_bank(("turned", i, h), after, [P, PER_HALF, P])
-            for b in range(PER_HALF):
-                c = h * PER_HALF + b
-                nc.tensor.transpose(bank[:, b, :], r_picked[i][:, c * P : (c + 1) * P], ident[:])
-            turned = keep.tile([P, PER_HALF, P], F32, name="r_by_edge%d_%d" % (i, h))
-            for b in range(PER_HALF):
-                c = h * PER_HALF + b
+        turned_banks = {}
+
+        def turn_r(k, after):
+            i, first, count = runs[k]
+            bank = take_bank(("turned", k), after, [P, count // P, P])
+            for b in range(count // P):
+                nc.tensor.transpose(bank[:, b, :], picked[i, first // P + b], ident[:])
+            turned_banks[k] = bank
+
+        def weigh_r(k):
+            i, first, count = runs[k]
+            bank = turned_banks[k]
+            turned = placed.tile([P, count // P, P], F32, name="r_by_edge%d" % k, offset=PLACES[k])
+            for b in range(count // P):
+                c = first // P + b
                 nc.scalar.activation(turned[:, b, :], bank[:, b, :], COPY, scale=edge_w[:, c : c + 1])
-            r_by_edge[i, h] = turned
+            r_by_edge[k] = turned
 
-        sums = [keep.tile([P, J], F32, name="sums%d" % i) for i in range(PACK)]
+        late_sums = [keep.tile([P, J], F32, name="sums%d" % i) for i in range(EARLY_PAGES, PACK)]
+        sums = {}
 
-        def add_and_turn_back(i, h, after):
-            bank = take_bank(("summed", i, h), after, [P, PER_HALF, P])
-            for b in range(PER_HALF):
-                terms = (r_by_edge[i, h][:, b, :], gated[h * PER_HALF + b][:, i, :])
-                for term, first in zip(terms, (True, False)):
-                    nc.tensor.matmul(bank[:, b, :], term, ident[:], start=first, stop=not first, is_transpose=True)
-            nc.scalar.copy(sums[i][:, h * HALF : (h + 1) * HALF], bank[:].rearrange("p b j -> p (b j)"))
+        def add_and_turn_back(k, after):
+            i, first, count = runs[k]
+            bank = take_bank(("summed", k), after, [P, count // P, P])
+            for b in range(count // P):
+                terms = (r_by_edge[k][:, b, :], gated[first // P + b][:, i, :])
+                for term, opens in zip(terms, (True, False)):
+                    nc.tensor.matmul(bank[:, b, :], term, ident[:], start=opens, stop=not opens, is_transpose=True)
+            if k == 0:
+                sums[k] = placed.tile([P, count], F32, name="first_sums", offset=HELD)[:]
+            elif i < EARLY_PAGES:
+                sums[k] = keep.tile([P, count], F32, name="sums_of_run%d" % k)[:]
+            else:
+                sums[k] = late_sums[i - EARLY_PAGES][:, first : first + count]
+            nc.scalar.copy(sums[k], bank[:].rearrange("p b j -> p (b j)"))
 
-        turn_r(0, 0, ("za", 3))
-        add_and_turn_back(0, 0, ("ms", 3))
-        gate(CHUNKS - 2, None, None)
-        gate(CHUNKS - 1, ("summed", 0, 0), ("ms", 4))
-        for i in range(EARLY_PAGES, PACK):
-            clear_page(nc.gpsimd)
-        turn_r(1, 0, ("ms", 6))
-        turn_r(0, 1, ("za", 5))
-        add_and_turn_back(1, 0, ("za", 4))
-        turn_r(1, 1, ("za", 6))
-        add_and_turn_back(0, 1, ("turned", 1, 0))
-        turn_r(2, 0, ("ms", 7))
-        add_and_turn_back(1, 1, ("za", 7))
-        turn_r(2, 1, ("summed", 1, 0))
-        add_and_turn_back(2, 0, ("ms", 5))
-        turn_r(3, 0, ("summed", 0, 1))
-        add_and_turn_back(2, 1, ("turned", 0, 0))
-        turn_r(3, 1, ("summed", 1, 1))
-        add_and_turn_back(3, 0, ("turned", 0, 1))
-        add_and_turn_back(3, 1, ("turned", 1, 1))
+        def scatter(i, first, values):
+            nc.vector.tensor_copy(pages[i][:].indirect(entries(tgt, first, values.shape[1])), values)
+
+        def step(k, before, piece):
+            add_and_turn_back(k, before)
+            if piece is not None:
+                gather_r(PACK - 1, piece * P, P, placed.tile([P, P], F32, name="piece%d" % k, offset=PLACES[k]))
+            if k < CHUNKS:
+                scatter(runs[k][0], runs[k][1], sums[k])
+
+        def turn_and_weigh(k, after):
+            turn_r(k, after)
+            weigh_r(k)
+
+        turn_and_weigh(0, ("ms", 1))
+        turn_r(1, ("za", 1))
+        step(0, None, None)
+        weigh_r(1)
+        step(1, ("summed", 0), 0)
+        gate(4, ("turned", 1), ("ms", 2))
+        turn_and_weigh(2, ("turned", 0))
+        turn_and_weigh(3, ("ms", 3))
+        step(2, ("summed", 1), 1)
+        gate(5, ("za", 4), ("ms", 4))
+        step(3, ("summed", 2), 2)
+        gate(6, ("turned", 2), ("turned", 3))
+        turn_and_weigh(4, ("za", 2))
+        turn_and_weigh(5, ("ms", 5))
+        gate(7, ("turned", 4), ("za", 5))
+        step(4, ("summed", 3), 3)
+        turn_and_weigh(6, ("ms", 6))
+        step(5, ("summed", 4), 4)
+        turn_and_weigh(7, ("za", 6))
+        turn_and_weigh(8, ("za", 3))
+        step(8, ("turned", 5), None)
+        step(6, ("summed", 5), 5)
+        turn_and_weigh(9, ("ms", 7))
+        step(7, ("summed", 6), 6)
+        step(9, ("summed", 7), 7)
+        turn_and_weigh(10, ("za", 7))
+        turn_and_weigh(11, ("summed", 9))
+        step(10, ("summed", 8), None)
+        step(11, ("turned", 9), None)
 
         out_rows = out_0.rearrange("(p i) t -> p i t", i=PACK)
         woven = [
@@ -261,17 +309,9 @@ def tile_list_rgg_LP_kernel(
             for q in range(PIECES)
         ]
 
-        def scatter(i, first, count):
-            places = pages[i][:].indirect(entries(tgt, first, count))
-            nc.vector.tensor_copy(places, sums[i][:, first : first + count])
-
-        for i in range(EARLY_PAGES):
-            scatter(i, 0, HALF)
         for i in range(PACK):
-            if i < EARLY_PAGES:
-                scatter(i, HALF, HALF)
-            else:
-                scatter(i, 0, J)
+            if i >= EARLY_PAGES:
+                scatter(i, 0, late_sums[i - EARLY_PAGES][:])
             nc.sync.dma_start(out_rows[:, i, :], pages[i][:])
             if i == PACK - 1:
                 break

@@ -136,6 +136,9 @@ def tile_list_rgg_LP_kernel(
             nc.tensor.transpose(w_bank[:], w_rows[:], ident[:])
             nc.scalar.copy(edge_w[:], w_bank[:, 0:CHUNKS])
 
+        warm = keep.tile([P, 1], F32, name="warm")
+        nc.scalar.activation(warm[:], ident[:, 0:1], SIGMOID)
+
         picked_plane = keep.tile([P, 2, J], U8, name="picked_plane", align_bytes=64)
         for side in (SRC, TGT):
             nc.vector.tensor_copy(picked_plane[:, side, :], tab_plane[:].indirect(lists[side][:]))
@@ -185,21 +188,15 @@ def tile_list_rgg_LP_kernel(
             nc.tensor.matmul_mx(ms[:], start=True, stop=True, **src_op, **wc_op)
             nc.tensor.matmul_mx(za[:], start=True, stop=False, **tgt_op, **wa_op)
             nc.tensor.matmul_mx(za[:], start=False, stop=True, **src_op, **wb_op)
-            if c == PER_HALF:
-                eta = placed.tile([P, PACK, P], F32, name="held_eta", offset=HELD + 1024)
-                msg = ring.tile([P, PACK, P], F32, name="msg")
-            else:
-                eta = ring.tile([P, PACK, P], F32, name="eta")
-                msg = ring.tile([P, PACK, P], F32, name="msg")
+            eta = ring.tile([P, PACK, P], F32, name="eta")
+            msg = ring.tile([P, PACK, P], F32, name="msg")
             nc.scalar.activation(eta[:], za[:].rearrange("j (m i) -> j i m", i=PACK), SIGMOID)
-            if c == 0:
-                turn_weights(("za", c))
             nc.scalar.activation(msg[:], ms[:].rearrange("j (m i) -> j i m", i=PACK), COPY, scale=edge_w[:, c : c + 1])
             nc.gpsimd.tensor_tensor(gated[c], msg[:], eta[:], MULT)
 
+        turn_weights(None)
         for c in range(CHUNKS_IN_PSUM):
             gate(c, None, None)
-        gate(CHUNKS_IN_PSUM, ("ms", 0), ("weights",))
 
         picked = {}
 
@@ -209,7 +206,7 @@ def tile_list_rgg_LP_kernel(
                 picked[i, first // P + b] = rows[:, b * P : (b + 1) * P]
 
         gather_r(0, 0, J, keep.tile([P, J], F32, name="picked0"))
-        gather_r(2, 0, J, keep.tile([P, J], F32, name="picked2"))
+        gather_r(2, 0, J - QUARTER, keep.tile([P, J - QUARTER], F32, name="picked2"))
         gather_r(1, 0, QUARTER, placed.tile([P, QUARTER], F32, name="picked1_first", offset=HELD + 512))
         gather_r(1, QUARTER, J - QUARTER, keep.tile([P, J - QUARTER], F32, name="picked1_rest"))
 
@@ -267,35 +264,37 @@ def tile_list_rgg_LP_kernel(
             turn_r(k, after)
             weigh_r(k)
 
-        turn_and_weigh(0, ("ms", 1))
-        turn_r(1, ("za", 1))
+        turn_and_weigh(0, ("weights",))
+        gate(3, ("ms", 0), ("za", 0))
+        turn_r(1, ("ms", 3))
+        gather_r(2, J - QUARTER, QUARTER, placed.tile([P, QUARTER], F32, name="picked2_last", offset=HELD + 1024))
         step(0, None, None)
         weigh_r(1)
-        step(1, ("summed", 0), 0)
-        gate(4, ("turned", 1), ("ms", 2))
-        turn_and_weigh(2, ("turned", 0))
-        turn_and_weigh(3, ("ms", 3))
-        step(2, ("summed", 1), 1)
-        gate(5, ("za", 4), ("ms", 4))
-        step(3, ("summed", 2), 2)
-        gate(6, ("turned", 2), ("turned", 3))
-        turn_and_weigh(4, ("za", 2))
-        turn_and_weigh(5, ("ms", 5))
-        gate(7, ("turned", 4), ("za", 5))
-        step(4, ("summed", 3), 3)
-        turn_and_weigh(6, ("ms", 6))
-        step(5, ("summed", 4), 4)
-        turn_and_weigh(7, ("za", 6))
-        turn_and_weigh(8, ("za", 3))
-        step(8, ("turned", 5), None)
-        step(6, ("summed", 5), 5)
-        turn_and_weigh(9, ("ms", 7))
-        step(7, ("summed", 6), 6)
+        step(1, ("turned", 0), 0)
+        gate(4, ("ms", 1), ("za", 1))
+        gate(5, ("ms", 2), ("za", 2))
+        turn_and_weigh(2, ("za", 3))
+        turn_and_weigh(3, ("ms", 4))
+        step(2, ("za", 4), 1)
+        gate(6, ("summed", 0), ("turned", 1))
+        turn_and_weigh(4, ("turned", 2))
+        step(3, ("summed", 1), 2)
+        gate(7, ("za", 6), ("ms", 6))
+        turn_and_weigh(5, ("turned", 3))
+        step(4, ("summed", 2), 3)
+        turn_and_weigh(6, ("turned", 4))
+        step(5, ("summed", 3), 4)
+        turn_and_weigh(7, ("turned", 5))
+        step(6, ("summed", 4), 5)
+        turn_and_weigh(8, ("ms", 7))
+        step(7, ("summed", 5), 6)
+        step(8, ("ms", 5), None)
+        turn_and_weigh(9, ("za", 7))
         step(9, ("summed", 7), 7)
-        turn_and_weigh(10, ("za", 7))
+        turn_and_weigh(10, ("turned", 8))
         turn_and_weigh(11, ("summed", 9))
         step(10, ("summed", 8), None)
-        step(11, ("turned", 9), None)
+        step(11, ("za", 5), None)
 
         out_rows = out_0.rearrange("(p i) t -> p i t", i=PACK)
         woven = [

@@ -29,8 +29,8 @@ EARLY_PAGES = 2
 LATE_CHUNKS = 2
 PIECE = 512
 PIECES = T // PIECE
-GPSIMD_PIECES = 3
-SPAN_WIDTHS = (512, 256, 256, 512, 256, 128, 128)
+GPSIMD_COLUMNS = 1280
+SPAN_WIDTHS = (512, 256, 256, 256, 256, 256, 128, 128)
 VECTOR_COLUMNS = 832
 STORE_ENDS = (768, 1536, 2048)
 RING = 6
@@ -297,16 +297,17 @@ def tile_list_rgg_LP_kernel(
         step(11, ("za", 5), None)
 
         out_rows = out_0.rearrange("(p i) t -> p i t", i=PACK)
+        shares = [(first, min(PIECE, GPSIMD_COLUMNS - first)) for first in range(0, GPSIMD_COLUMNS, PIECE)]
         woven = [
-            keep.tile(
-                [P, PIECE, PACK],
-                BF16,
-                name="woven%d" % q,
-                tag="woven%d" % q if q < GPSIMD_PIECES else "gated_then_woven%d" % q,
-                align_bytes=64,
-            )
-            for q in range(PIECES)
+            keep.tile([P, width, PACK], BF16, name="woven%d" % q, align_bytes=64) for q, (first, width) in enumerate(shares)
         ]
+        shares.append((GPSIMD_COLUMNS, T - GPSIMD_COLUMNS))
+        last_tag = "gated_then_woven%d" % (CHUNKS // 2 - 1)
+        woven.append(keep.tile([P, T - GPSIMD_COLUMNS, PACK], BF16, name="woven_last", tag=last_tag, align_bytes=64))
+
+        def woven_columns(first, end):
+            q = max(n for n, (start, width) in enumerate(shares) if start <= first)
+            return woven[q][:, first - shares[q][0] : end - shares[q][0], :]
 
         for i in range(PACK):
             if i >= EARLY_PAGES:
@@ -314,12 +315,12 @@ def tile_list_rgg_LP_kernel(
             nc.sync.dma_start(out_rows[:, i, :], pages[i][:])
             if i == PACK - 1:
                 break
-            for q in range(PIECES):
-                piece = pages[i][:, q * PIECE : (q + 1) * PIECE]
-                if q >= GPSIMD_PIECES:
+            for q, (first, width) in enumerate(shares):
+                piece = pages[i][:, first : first + width]
+                if first >= GPSIMD_COLUMNS:
                     nc.scalar.copy(woven[q][:, :, i], piece)
                 elif i == PACK - 2:
-                    twice = piece.unsqueeze(2).to_broadcast([P, PIECE, 2])
+                    twice = piece.unsqueeze(2).to_broadcast([P, width, 2])
                     nc.gpsimd.tensor_scalar(woven[q][:, :, i:], twice, 1.0, 0.0, MULT, ADD)
                 else:
                     nc.gpsimd.tensor_scalar(woven[q][:, :, i], piece, 1.0, 0.0, MULT, ADD)
@@ -330,8 +331,7 @@ def tile_list_rgg_LP_kernel(
         spans = [(sum(SPAN_WIDTHS[:s]), width) for s, width in enumerate(SPAN_WIDTHS)]
         cuts = sorted(set([first for first, width in spans] + [VECTOR_COLUMNS, T]))
         for first, end in zip(cuts, cuts[1:]):
-            q, inner = divmod(first, PIECE)
-            dst = woven[q][:, inner : inner + end - first, PACK - 1]
+            dst = woven_columns(first, end)[:, :, PACK - 1]
             if first < VECTOR_COLUMNS:
                 nc.vector.tensor_copy(dst, pages[PACK - 1][:, first:end])
             else:
@@ -340,7 +340,7 @@ def tile_list_rgg_LP_kernel(
         for first, width in spans:
             q, inner = divmod(first, PIECE)
             cols = slice(first, first + width)
-            span = woven[q][:, inner : inner + width, :].rearrange("p c i -> p (c i)")
+            span = woven_columns(first, first + width).rearrange("p c i -> p (c i)")
             nc.vector.quantize_mx(out_codes[:, cols].bitcast(FP8X4), out_plane[4 * q :, inner : inner + width], span)
             if cols.stop in STORE_ENDS:
                 nc.sync.dma_start(out_words[:, stored : cols.stop], out_codes[:, stored : cols.stop])

@@ -26,7 +26,7 @@ HALF = J // 2
 CHUNKS = J // P
 PER_HALF = HALF // P
 EARLY_PAGES = 2
-LATE_CHUNKS = 2
+LATE_CHUNKS = 3
 PIECE = 512
 PIECES = T // PIECE
 GPSIMD_COLUMNS = 1280
@@ -37,8 +37,9 @@ RING = 6
 CHUNKS_IN_PSUM = 3
 SYNC_WA_QUADRANTS = 2
 QUARTER = J // 4
-PLACES = (0, 1024, 1536, 6144, 2048, 6656, 2560, 7168, 3072, 7680, 10240, 12288)
-HELD = 14336
+PLACES = dict(enumerate((0, 1024, 1536, 6144, 2048, 6656, 2560, 7168, 3072, 7680, 10240, 12288)))
+AHEAD = 14336
+HELD = 14848
 SRC, TGT = 0, 1
 WA, WC = 0, 1
 
@@ -112,7 +113,7 @@ def tile_list_rgg_LP_kernel(
         load_quadrants(w_planes[:, WA, :], wa_scales, nc.gpsimd, range(SYNC_WA_QUADRANTS, QUADRANTS))
         r_rows = rT.rearrange("(p i) t -> p i t", i=PACK)
         r_all = [keep.tile([P, T], F32, name="r_all%d" % i) for i in range(PACK)]
-        for i in (0, 2, 1, 3):
+        for i in range(PACK):
             nc.sync.dma_start(r_all[i][:], r_rows[:, i, :])
 
         ident = keep.tile([P, P], F32, name="ident")
@@ -127,7 +128,6 @@ def tile_list_rgg_LP_kernel(
 
         clear_page(nc.vector, "page0")
         clear_page(nc.gpsimd, "page1")
-        clear_page(nc.gpsimd, "page2")
 
         edge_w = keep.tile([P, CHUNKS], F32, name="edge_w")
 
@@ -166,7 +166,6 @@ def tile_list_rgg_LP_kernel(
             nc.vector.quantize_mx(wb_codes[:, cols].bitcast(FP8X4), wb_plane[:, cols], grouped)
 
         gather_words(1, "wb_raw1")
-        clear_page(nc.gpsimd, "wb_bf1")
 
         two_chunks = [
             keep.tile([P, 2, PACK, P], F32, name="gated%d" % q, tag="gated_then_woven%d" % q, align_bytes=64)
@@ -188,8 +187,15 @@ def tile_list_rgg_LP_kernel(
             nc.tensor.matmul_mx(ms[:], start=True, stop=True, **src_op, **wc_op)
             nc.tensor.matmul_mx(za[:], start=True, stop=False, **tgt_op, **wa_op)
             nc.tensor.matmul_mx(za[:], start=False, stop=True, **src_op, **wb_op)
-            eta = ring.tile([P, PACK, P], F32, name="eta")
-            msg = ring.tile([P, PACK, P], F32, name="msg")
+            if c == CHUNKS - 1:
+                eta = keep.tile([P, PACK, P], F32, name="last_eta", tag="page2", align_bytes=64)
+                msg = keep.tile([P, PACK, P], F32, name="last_msg", tag="page3", align_bytes=64)
+            elif c == CHUNKS - LATE_CHUNKS:
+                eta = placed.tile([P, PACK, P], F32, name="held_eta", offset=HELD + 1024)
+                msg = ring.tile([P, PACK, P], F32, name="msg")
+            else:
+                eta = ring.tile([P, PACK, P], F32, name="eta")
+                msg = ring.tile([P, PACK, P], F32, name="msg")
             nc.scalar.activation(eta[:], za[:].rearrange("j (m i) -> j i m", i=PACK), SIGMOID)
             nc.scalar.activation(msg[:], ms[:].rearrange("j (m i) -> j i m", i=PACK), COPY, scale=edge_w[:, c : c + 1])
             nc.gpsimd.tensor_tensor(gated[c], msg[:], eta[:], MULT)
@@ -206,31 +212,34 @@ def tile_list_rgg_LP_kernel(
                 picked[i, first // P + b] = rows[:, b * P : (b + 1) * P]
 
         gather_r(0, 0, J, keep.tile([P, J], F32, name="picked0"))
-        gather_r(2, 0, J - QUARTER, keep.tile([P, J - QUARTER], F32, name="picked2"))
-        gather_r(1, 0, QUARTER, placed.tile([P, QUARTER], F32, name="picked1_first", offset=HELD + 512))
-        gather_r(1, QUARTER, J - QUARTER, keep.tile([P, J - QUARTER], F32, name="picked1_rest"))
+        gather_r(1, 0, J, keep.tile([P, J], F32, name="picked1"))
+        gather_r(2, 0, P, placed.tile([P, P], F32, name="picked2_first", offset=HELD + 768))
+        gather_r(2, P, J - P, keep.tile([P, J - P], F32, name="picked2_rest"))
 
         runs = [(i, first, QUARTER) for first in range(0, J, QUARTER) for i in range(EARLY_PAGES)]
         runs += [(i, first, HALF) for i in range(EARLY_PAGES, PACK) for first in range(0, J, HALF)]
+        turns = dict(enumerate(runs))
+        turns[CHUNKS] = (EARLY_PAGES, P, HALF - P)
+        turns["ahead"] = (EARLY_PAGES, 0, P)
         r_by_edge = {}
 
         turned_banks = {}
 
         def turn_r(k, after):
-            i, first, count = runs[k]
+            i, first, count = turns[k]
             bank = take_bank(("turned", k), after, [P, count // P, P])
             for b in range(count // P):
                 nc.tensor.transpose(bank[:, b, :], picked[i, first // P + b], ident[:])
             turned_banks[k] = bank
 
         def weigh_r(k):
-            i, first, count = runs[k]
+            i, first, count = turns[k]
             bank = turned_banks[k]
-            turned = placed.tile([P, count // P, P], F32, name="r_by_edge%d" % k, offset=PLACES[k])
+            turned = placed.tile([P, count // P, P], F32, name="r_by_edge%s" % k, offset=PLACES.get(k, AHEAD))
             for b in range(count // P):
                 c = first // P + b
                 nc.scalar.activation(turned[:, b, :], bank[:, b, :], COPY, scale=edge_w[:, c : c + 1])
-            r_by_edge[k] = turned
+                r_by_edge[i, c] = turned[:, b, :]
 
         late_sums = [keep.tile([P, J], F32, name="sums%d" % i) for i in range(EARLY_PAGES, PACK)]
         sums = {}
@@ -239,7 +248,7 @@ def tile_list_rgg_LP_kernel(
             i, first, count = runs[k]
             bank = take_bank(("summed", k), after, [P, count // P, P])
             for b in range(count // P):
-                terms = (r_by_edge[k][:, b, :], gated[first // P + b][:, i, :])
+                terms = (r_by_edge[i, first // P + b], gated[first // P + b][:, i, :])
                 for term, opens in zip(terms, (True, False)):
                     nc.tensor.matmul(bank[:, b, :], term, ident[:], start=opens, stop=not opens, is_transpose=True)
             if k == 0:
@@ -266,35 +275,37 @@ def tile_list_rgg_LP_kernel(
 
         turn_and_weigh(0, ("weights",))
         gate(3, ("ms", 0), ("za", 0))
-        turn_r(1, ("ms", 3))
-        gather_r(2, J - QUARTER, QUARTER, placed.tile([P, QUARTER], F32, name="picked2_last", offset=HELD + 1024))
+        turn_r("ahead", ("turned", 0))
         step(0, None, None)
-        weigh_r(1)
-        step(1, ("turned", 0), 0)
+        turn_and_weigh(1, ("ms", 3))
+        step(1, ("summed", 0), 0)
+        weigh_r("ahead")
         gate(4, ("ms", 1), ("za", 1))
-        gate(5, ("ms", 2), ("za", 2))
         turn_and_weigh(2, ("za", 3))
-        turn_and_weigh(3, ("ms", 4))
         step(2, ("za", 4), 1)
-        gate(6, ("summed", 0), ("turned", 1))
-        turn_and_weigh(4, ("turned", 2))
+        gate(5, ("turned", "ahead"), ("za", 2))
+        turn_and_weigh(3, ("za", 5))
         step(3, ("summed", 1), 2)
-        gate(7, ("za", 6), ("ms", 6))
+        gate(6, ("turned", 2), ("ms", 5))
+        turn_and_weigh(4, ("ms", 6))
+        gate(7, ("turned", 4), ("za", 6))
+        for i in range(EARLY_PAGES, PACK):
+            clear_page(nc.gpsimd, "page%d" % i)
         turn_and_weigh(5, ("turned", 3))
         step(4, ("summed", 2), 3)
-        turn_and_weigh(6, ("turned", 4))
+        turn_and_weigh(6, ("ms", 4))
         step(5, ("summed", 3), 4)
         turn_and_weigh(7, ("turned", 5))
         step(6, ("summed", 4), 5)
         turn_and_weigh(8, ("ms", 7))
         step(7, ("summed", 5), 6)
-        step(8, ("ms", 5), None)
+        step(8, ("turned", 1), None)
         turn_and_weigh(9, ("za", 7))
         step(9, ("summed", 7), 7)
         turn_and_weigh(10, ("turned", 8))
         turn_and_weigh(11, ("summed", 9))
         step(10, ("summed", 8), None)
-        step(11, ("za", 5), None)
+        step(11, ("ms", 2), None)
 
         out_rows = out_0.rearrange("(p i) t -> p i t", i=PACK)
         shares = [(first, min(PIECE, GPSIMD_COLUMNS - first)) for first in range(0, GPSIMD_COLUMNS, PIECE)]

@@ -37,7 +37,7 @@ RING = 6
 CHUNKS_IN_PSUM = 3
 SYNC_WA_QUADRANTS = 2
 QUARTER = J // 4
-PLACES = dict(enumerate((0, 1024, 1536, 6144, 2048, 6656, 2560, 7168, 3072, 7680, 10240, 12288)))
+PLACES = dict(enumerate((0, 5632, 512, 6144, 1024, 6656, 1536, 7168, 2048, 7680, 10240, 12288)))
 AHEAD = 14336
 HELD = 14848
 SRC, TGT = 0, 1
@@ -278,27 +278,27 @@ def tile_list_rgg_LP_kernel(
         turn_r("ahead", ("turned", 0))
         step(0, None, None)
         turn_and_weigh(1, ("ms", 3))
-        step(1, ("summed", 0), 0)
         weigh_r("ahead")
+        step(1, ("turned", "ahead"), 0)
         gate(4, ("ms", 1), ("za", 1))
         turn_and_weigh(2, ("za", 3))
-        step(2, ("za", 4), 1)
-        gate(5, ("turned", "ahead"), ("za", 2))
+        step(2, ("summed", 0), 1)
+        gate(5, ("summed", 1), ("za", 2))
         turn_and_weigh(3, ("za", 5))
-        step(3, ("summed", 1), 2)
-        gate(6, ("turned", 2), ("ms", 5))
-        turn_and_weigh(4, ("ms", 6))
+        step(3, ("za", 4), 2)
+        gate(6, ("summed", 2), ("ms", 5))
+        turn_and_weigh(4, ("turned", 2))
         gate(7, ("turned", 4), ("za", 6))
         for i in range(EARLY_PAGES, PACK):
             clear_page(nc.gpsimd, "page%d" % i)
         turn_and_weigh(5, ("turned", 3))
-        step(4, ("summed", 2), 3)
+        step(4, ("ms", 6), 3)
         turn_and_weigh(6, ("ms", 4))
-        step(5, ("summed", 3), 4)
+        step(5, ("summed", 4), 4)
         turn_and_weigh(7, ("turned", 5))
-        step(6, ("summed", 4), 5)
+        step(6, ("summed", 3), 5)
         turn_and_weigh(8, ("ms", 7))
-        step(7, ("summed", 5), 6)
+        step(7, ("summed", 6), 6)
         step(8, ("turned", 1), None)
         turn_and_weigh(9, ("za", 7))
         step(9, ("summed", 7), 7)

@@ -31,8 +31,8 @@ PIECE = 512
 PIECES = T // PIECE
 GPSIMD_COLUMNS = 1280
 SPAN_WIDTHS = (512, 256, 256, 256, 256, 256, 128, 128)
-VECTOR_COLUMNS = 832
-STORE_ENDS = (768, 1536, 2048)
+VECTOR_COLUMNS = 960
+STORE_ENDS = (512, 1024, 1536, 1920, 2048)
 RING = 6
 CHUNKS_IN_PSUM = 3
 SYNC_WA_QUADRANTS = 2
@@ -341,14 +341,22 @@ def tile_list_rgg_LP_kernel(
         out_words = words_of(out_1)
         spans = [(sum(SPAN_WIDTHS[:s]), width) for s, width in enumerate(SPAN_WIDTHS)]
         cuts = sorted(set([first for first, width in spans] + [VECTOR_COLUMNS, T]))
-        for first, end in zip(cuts, cuts[1:]):
+        copies = list(zip(cuts, cuts[1:]))
+
+        def round_last(first, end):
             dst = woven_columns(first, end)[:, :, PACK - 1]
             if first < VECTOR_COLUMNS:
                 nc.vector.tensor_copy(dst, pages[PACK - 1][:, first:end])
             else:
                 nc.scalar.copy(dst, pages[PACK - 1][:, first:end])
+
         stored = 0
+        rounded = 0
         for first, width in spans:
+            ahead = [n for n, (start, end) in enumerate(copies) if start < first + width][-1] + 2
+            for start, end in copies[rounded:ahead]:
+                round_last(start, end)
+            rounded = max(rounded, ahead)
             q, inner = divmod(first, PIECE)
             cols = slice(first, first + width)
             span = woven_columns(first, first + width).rearrange("p c i -> p (c i)")

@@ -37,9 +37,10 @@ RING = 6
 CHUNKS_IN_PSUM = 3
 SYNC_WA_QUADRANTS = 2
 QUARTER = J // 4
-PLACES = dict(enumerate((0, 5632, 512, 6144, 1024, 6656, 1536, 7168, 2048, 7680, 10240, 12288)))
+PLACES = dict(enumerate([6144 * (k % 2) + 512 * (k // 2) for k in range(14)]))
 AHEAD = 14336
 HELD = 14848
+HEAD_COLUMNS = 768
 SRC, TGT = 0, 1
 WA, WC = 0, 1
 
@@ -121,13 +122,15 @@ def tile_list_rgg_LP_kernel(
 
         pages = []
 
-        def clear_page(engine, tag):
+        def clear_page(engine, tag, columns=T):
             page = keep.tile([P, T], F32, name="page%d" % len(pages), tag=tag, align_bytes=64)
-            engine.memset(page[:], 0.0)
+            engine.memset(page[:, :columns], 0.0)
             pages.append(page)
 
         clear_page(nc.vector, "page0")
         clear_page(nc.gpsimd, "page1")
+        clear_page(nc.vector, "page2", HEAD_COLUMNS)
+        nc.gpsimd.memset(pages[2][:, HEAD_COLUMNS:], 0.0)
 
         edge_w = keep.tile([P, CHUNKS], F32, name="edge_w")
 
@@ -188,7 +191,7 @@ def tile_list_rgg_LP_kernel(
             nc.tensor.matmul_mx(za[:], start=True, stop=False, **tgt_op, **wa_op)
             nc.tensor.matmul_mx(za[:], start=False, stop=True, **src_op, **wb_op)
             if c == CHUNKS - 1:
-                eta = keep.tile([P, PACK, P], F32, name="last_eta", tag="page2", align_bytes=64)
+                eta = keep.tile([P, PACK, P], F32, name="last_eta")
                 msg = keep.tile([P, PACK, P], F32, name="last_msg", tag="page3", align_bytes=64)
             elif c == CHUNKS - LATE_CHUNKS:
                 eta = placed.tile([P, PACK, P], F32, name="held_eta", offset=HELD + 1024)
@@ -212,14 +215,16 @@ def tile_list_rgg_LP_kernel(
                 picked[i, first // P + b] = rows[:, b * P : (b + 1) * P]
 
         gather_r(0, 0, J, keep.tile([P, J], F32, name="picked0"))
-        gather_r(1, 0, J, keep.tile([P, J], F32, name="picked1"))
+        gather_r(1, 0, J - QUARTER, keep.tile([P, J - QUARTER], F32, name="picked1"))
         gather_r(2, 0, P, placed.tile([P, P], F32, name="picked2_first", offset=HELD + 768))
         gather_r(2, P, J - P, keep.tile([P, J - P], F32, name="picked2_rest"))
 
-        runs = [(i, first, QUARTER) for first in range(0, J, QUARTER) for i in range(EARLY_PAGES)]
-        runs += [(i, first, HALF) for i in range(EARLY_PAGES, PACK) for first in range(0, J, HALF)]
+        quarters = [(0, 0), (1, 0), (0, 1), (1, 1), (0, 2), (2, 0), (0, 3), (1, 2), (2, 1), (1, 3)]
+        runs = [(i, q * QUARTER, QUARTER) for i, q in quarters]
+        runs += [(2, HALF, HALF), (3, 0, HALF), (3, HALF, QUARTER), (3, J - QUARTER, QUARTER)]
+        pieces = [(1, CHUNKS - 2), (1, CHUNKS - 1)] + [(PACK - 1, c) for c in range(CHUNKS)]
         turns = dict(enumerate(runs))
-        turns[CHUNKS] = (EARLY_PAGES, P, HALF - P)
+        turns[5] = (EARLY_PAGES, P, P)
         turns["ahead"] = (EARLY_PAGES, 0, P)
         r_by_edge = {}
 
@@ -235,13 +240,14 @@ def tile_list_rgg_LP_kernel(
         def weigh_r(k):
             i, first, count = turns[k]
             bank = turned_banks[k]
-            turned = placed.tile([P, count // P, P], F32, name="r_by_edge%s" % k, offset=PLACES.get(k, AHEAD))
+            blocks = runs[k][2] // P if k in PLACES else 1
+            turned = placed.tile([P, blocks, P], F32, name="r_by_edge%s" % k, offset=PLACES.get(k, AHEAD))
             for b in range(count // P):
                 c = first // P + b
                 nc.scalar.activation(turned[:, b, :], bank[:, b, :], COPY, scale=edge_w[:, c : c + 1])
                 r_by_edge[i, c] = turned[:, b, :]
 
-        late_sums = [keep.tile([P, J], F32, name="sums%d" % i) for i in range(EARLY_PAGES, PACK)]
+        last_sums = keep.tile([P, J], F32, name="last_sums")
         sums = {}
 
         def add_and_turn_back(k, after):
@@ -253,10 +259,10 @@ def tile_list_rgg_LP_kernel(
                     nc.tensor.matmul(bank[:, b, :], term, ident[:], start=opens, stop=not opens, is_transpose=True)
             if k == 0:
                 sums[k] = placed.tile([P, count], F32, name="first_sums", offset=HELD)[:]
-            elif i < EARLY_PAGES:
+            elif i < PACK - 1:
                 sums[k] = keep.tile([P, count], F32, name="sums_of_run%d" % k)[:]
             else:
-                sums[k] = late_sums[i - EARLY_PAGES][:, first : first + count]
+                sums[k] = last_sums[:, first : first + count]
             nc.scalar.copy(sums[k], bank[:].rearrange("p b j -> p (b j)"))
 
         def scatter(i, first, values):
@@ -265,8 +271,9 @@ def tile_list_rgg_LP_kernel(
         def step(k, before, piece):
             add_and_turn_back(k, before)
             if piece is not None:
-                gather_r(PACK - 1, piece * P, P, placed.tile([P, P], F32, name="piece%d" % k, offset=PLACES[k]))
-            if k < CHUNKS:
+                i, c = pieces[piece]
+                gather_r(i, c * P, P, placed.tile([P, P], F32, name="piece%d" % k, offset=PLACES[k]))
+            if runs[k][0] < PACK - 1:
                 scatter(runs[k][0], runs[k][1], sums[k])
 
         def turn_and_weigh(k, after):
@@ -289,8 +296,7 @@ def tile_list_rgg_LP_kernel(
         gate(6, ("summed", 2), ("ms", 5))
         turn_and_weigh(4, ("turned", 2))
         gate(7, ("turned", 4), ("za", 6))
-        for i in range(EARLY_PAGES, PACK):
-            clear_page(nc.gpsimd, "page%d" % i)
+        clear_page(nc.gpsimd, "page3")
         turn_and_weigh(5, ("turned", 3))
         step(4, ("ms", 6), 3)
         turn_and_weigh(6, ("ms", 4))
@@ -299,13 +305,17 @@ def tile_list_rgg_LP_kernel(
         step(6, ("summed", 3), 5)
         turn_and_weigh(8, ("ms", 7))
         step(7, ("summed", 6), 6)
-        step(8, ("turned", 1), None)
         turn_and_weigh(9, ("za", 7))
-        step(9, ("summed", 7), 7)
+        step(8, ("summed", 7), 7)
         turn_and_weigh(10, ("turned", 8))
-        turn_and_weigh(11, ("summed", 9))
-        step(10, ("summed", 8), None)
+        step(9, ("summed", 8), 8)
+        turn_and_weigh(11, ("turned", 9))
+        step(10, ("summed", 9), 9)
         step(11, ("ms", 2), None)
+        turn_and_weigh(12, ("turned", 11))
+        step(12, ("turned", 10), None)
+        turn_and_weigh(13, ("turned", 12))
+        step(13, ("summed", 10), None)
 
         out_rows = out_0.rearrange("(p i) t -> p i t", i=PACK)
         shares = [(first, min(PIECE, GPSIMD_COLUMNS - first)) for first in range(0, GPSIMD_COLUMNS, PIECE)]
@@ -321,8 +331,8 @@ def tile_list_rgg_LP_kernel(
             return woven[q][:, first - shares[q][0] : end - shares[q][0], :]
 
         for i in range(PACK):
-            if i >= EARLY_PAGES:
-                scatter(i, 0, late_sums[i - EARLY_PAGES][:])
+            if i == PACK - 1:
+                scatter(i, 0, last_sums[:])
             nc.sync.dma_start(out_rows[:, i, :], pages[i][:])
             if i == PACK - 1:
                 break

@@ -31,13 +31,13 @@ PIECE = 512
 PIECES = T // PIECE
 GPSIMD_COLUMNS = 1280
 SPAN_WIDTHS = (512, 256, 256, 256, 256, 256, 128, 128)
-VECTOR_COLUMNS = 960
+VECTOR_COLUMNS = 1024
 STORE_ENDS = (512, 1024, 1536, 1920, 2048)
 RING = 6
 CHUNKS_IN_PSUM = 3
 SYNC_WA_QUADRANTS = 2
 QUARTER = J // 4
-PLACES = dict(enumerate([6144 * (k % 2) + 512 * (k // 2) for k in range(14)]))
+PLACES = dict(enumerate([6144 * (k % 2) + 512 * (k // 2) for k in range(14)] + [12288]))
 AHEAD = 14336
 HELD = 14848
 HEAD_COLUMNS = 768
@@ -221,7 +221,7 @@ def tile_list_rgg_LP_kernel(
 
         quarters = [(0, 0), (1, 0), (0, 1), (1, 1), (0, 2), (2, 0), (0, 3), (1, 2), (2, 1), (1, 3)]
         runs = [(i, q * QUARTER, QUARTER) for i, q in quarters]
-        runs += [(2, HALF, HALF), (3, 0, HALF), (3, HALF, QUARTER), (3, J - QUARTER, QUARTER)]
+        runs += [(2, J - QUARTER, QUARTER), (3, 0, HALF), (3, HALF, HALF - P), (3, J - P, P), (2, HALF, QUARTER)]
         pieces = [(1, CHUNKS - 2), (1, CHUNKS - 1)] + [(PACK - 1, c) for c in range(CHUNKS)]
         turns = dict(enumerate(runs))
         turns[5] = (EARLY_PAGES, P, P)
@@ -248,6 +248,7 @@ def tile_list_rgg_LP_kernel(
                 r_by_edge[i, c] = turned[:, b, :]
 
         last_sums = keep.tile([P, J], F32, name="last_sums")
+        half_sums = keep.tile([P, HALF], F32, name="half_sums")
         sums = {}
 
         def add_and_turn_back(k, after):
@@ -259,6 +260,8 @@ def tile_list_rgg_LP_kernel(
                     nc.tensor.matmul(bank[:, b, :], term, ident[:], start=opens, stop=not opens, is_transpose=True)
             if k == 0:
                 sums[k] = placed.tile([P, count], F32, name="first_sums", offset=HELD)[:]
+            elif i == EARLY_PAGES and first >= HALF:
+                sums[k] = half_sums[:, first - HALF : first - HALF + count]
             elif i < PACK - 1:
                 sums[k] = keep.tile([P, count], F32, name="sums_of_run%d" % k)[:]
             else:
@@ -273,7 +276,7 @@ def tile_list_rgg_LP_kernel(
             if piece is not None:
                 i, c = pieces[piece]
                 gather_r(i, c * P, P, placed.tile([P, P], F32, name="piece%d" % k, offset=PLACES[k]))
-            if runs[k][0] < PACK - 1:
+            if k < len(quarters):
                 scatter(runs[k][0], runs[k][1], sums[k])
 
         def turn_and_weigh(k, after):
@@ -307,10 +310,13 @@ def tile_list_rgg_LP_kernel(
         step(7, ("summed", 6), 6)
         turn_and_weigh(9, ("za", 7))
         step(8, ("summed", 7), 7)
+        turn_and_weigh(14, ("summed", 5))
+        step(14, ("turned", 14), None)
         turn_and_weigh(10, ("turned", 8))
         step(9, ("summed", 8), 8)
         turn_and_weigh(11, ("turned", 9))
         step(10, ("summed", 9), 9)
+        scatter(EARLY_PAGES, HALF, half_sums[:])
         step(11, ("ms", 2), None)
         turn_and_weigh(12, ("turned", 11))
         step(12, ("turned", 10), None)

@@ -26,12 +26,12 @@ HALF = J // 2
 CHUNKS = J // P
 PER_HALF = HALF // P
 EARLY_PAGES = 2
-LATE_CHUNKS = 3
+LATE_CHUNKS = 4
 PIECE = 512
 PIECES = T // PIECE
 GPSIMD_COLUMNS = 1280
 SPAN_WIDTHS = (512, 256, 256, 256, 256, 256, 128, 128)
-VECTOR_COLUMNS = 1024
+VECTOR_COLUMNS = 960
 STORE_ENDS = (512, 1024, 1536, 1920, 2048)
 RING = 6
 CHUNKS_IN_PSUM = 3

from contextlib import ExitStack

import concourse.mybir as mybir
from concourse.masks import make_identity

K, N, T, J = 512, 512, 2048, 1024
FLOPS = 3 * 2 * K * N * J

F32 = mybir.dt.float32
BF16 = mybir.dt.bfloat16
I32 = mybir.dt.int32
U32 = mybir.dt.uint32
U16 = mybir.dt.uint16
U8 = mybir.dt.uint8
FP8X4 = mybir.dt.float8_e4m3fn_x4
MULT = mybir.AluOpType.mult
ADD = mybir.AluOpType.add
COPY = mybir.ActivationFunctionType.Copy
SIGMOID = mybir.ActivationFunctionType.Sigmoid

P = 128
PACK = 4
QUADRANTS = 4
LIST_ROWS = 16
HALF = J // 2
CHUNKS = J // P
PER_HALF = HALF // P
EARLY_PAGES = 2
LATE_CHUNKS = 4
PIECE = 512
PIECES = T // PIECE
GPSIMD_COLUMNS = 1280
SPAN_WIDTHS = (512, 256, 256, 256, 256, 256, 128, 128)
VECTOR_COLUMNS = 960
STORE_ENDS = (512, 1024, 1536, 1920, 2048)
RING = 6
CHUNKS_IN_PSUM = 3
SYNC_WA_QUADRANTS = 2
QUARTER = J // 4
PLACES = dict(enumerate([6144 * (k % 2) + 512 * (k // 2) for k in range(14)] + [12288]))
AHEAD = 14336
HELD = 14848
HEAD_COLUMNS = 768
SRC, TGT = 0, 1
WA, WC = 0, 1


def tile_list_rgg_LP_kernel(
    tc, tab_words, tab_scales, wa_words, wa_scales, wb, wc_words, wc_scales, rT, wgo, offs, offs2, out_0, out_1, out_2
):
    nc = tc.nc
    with ExitStack() as ctx:
        keep = ctx.enter_context(tc.tile_pool(name="keep", bufs=1))
        ring = ctx.enter_context(tc.tile_pool(name="ring", bufs=RING))
        placed = ctx.enter_context(tc.tile_pool(name="placed", bufs=1))
        psum = ctx.enter_context(tc.psum_pool(name="psum", bufs=1))

        bank_of = {}
        opened = []

        def take_bank(user, after, shape):
            if after is None:
                bank_of[user] = len(opened)
                opened.append(user)
            else:
                bank_of[user] = bank_of[after]
            return psum.tile(shape, F32, name=user[0], tag="bank%d" % bank_of[user])

        def load_plane(plane, scales, queue, rows):
            for r in rows:
                queue.dma_start(plane[r:P:32, :].bitcast(I32), scales[0, r : 4 * QUADRANTS : 4, :].bitcast(I32))

        def load_quadrants(plane, scales, queue, quads):
            for quad in quads:
                rows = scales[0, 4 * quad : 4 * quad + 4, :].bitcast(I32)
                queue.dma_start(plane[32 * quad : 32 * quad + 4, :].bitcast(I32), rows)

        def words_of(packed):
            return packed[0].rearrange("p c i -> p (c i)").bitcast(I32)

        def entries(lst, first, count):
            return lst[:, first // LIST_ROWS : (first + count) // LIST_ROWS]

        src = keep.tile([P, J // LIST_ROWS], U16, name="src")
        tgt = keep.tile([P, J // LIST_ROWS], U16, name="tgt")
        nc.sync.dma_start(src[:], offs)
        nc.sync.dma_start(tgt[:], offs2)
        lists = (src, tgt)

        tab_plane = keep.tile([P, T], U8, name="tab_plane", align_bytes=64)
        w_planes = keep.tile([P, 2, N], U8, name="w_planes", align_bytes=64)
        nc.gpsimd.memset(tab_plane[:].bitcast(I32), 0)
        nc.gpsimd.memset(w_planes[:].rearrange("p w n -> p (w n)").bitcast(I32), 0)
        w_rows = keep.tile([P, P], F32, name="w_rows")
        nc.gpsimd.memset(w_rows[:], 0.0)
        load_plane(tab_plane, tab_scales, nc.sync, range(QUADRANTS))
        tab_codes = keep.tile([P, T], I32, name="tab_codes", align_bytes=64)
        nc.sync.dma_start(tab_codes[:], words_of(tab_words))
        load_quadrants(w_planes[:, WA, :], wa_scales, nc.sync, range(SYNC_WA_QUADRANTS))

        wb_rows = wb.rearrange("(p i) n -> p i n", i=PACK)
        wb_cols = [slice(0, N // 2), slice(N // 2, N)]
        wb_raw = []
        for u, cols in enumerate(wb_cols):
            part = keep.tile([P, PACK, N // 2], F32, name="wb_raw%d" % u, tag="wb_raw%d" % u, align_bytes=64)
            nc.sync.dma_start(part[:], wb_rows[:, :, cols])
            wb_raw.append(part)
        wa_codes = keep.tile([P, N], I32, name="wa_codes", align_bytes=64)
        wc_codes = keep.tile([P, N], I32, name="wc_codes", align_bytes=64)
        load_quadrants(w_planes[:, WC, :], wc_scales, nc.sync, range(QUADRANTS))
        nc.gpsimd.dma_start(w_rows[0:CHUNKS, :], wgo[0:1, :].rearrange("o (c j) -> (o c) j", j=P))
        nc.sync.dma_start(wc_codes[:], words_of(wc_words))
        nc.sync.dma_start(wa_codes[:], words_of(wa_words))
        load_quadrants(w_planes[:, WA, :], wa_scales, nc.gpsimd, range(SYNC_WA_QUADRANTS, QUADRANTS))
        r_rows = rT.rearrange("(p i) t -> p i t", i=PACK)
        r_all = [keep.tile([P, T], F32, name="r_all%d" % i) for i in range(PACK)]
        for i in range(PACK):
            nc.sync.dma_start(r_all[i][:], r_rows[:, i, :])

        ident = keep.tile([P, P], F32, name="ident")
        make_identity(nc, ident[:])

        pages = []

        def clear_page(engine, tag, columns=T):
            page = keep.tile([P, T], F32, name="page%d" % len(pages), tag=tag, align_bytes=64)
            engine.memset(page[:, :columns], 0.0)
            pages.append(page)

        clear_page(nc.vector, "page0")
        clear_page(nc.gpsimd, "page1")
        clear_page(nc.vector, "page2", HEAD_COLUMNS)
        nc.gpsimd.memset(pages[2][:, HEAD_COLUMNS:], 0.0)

        edge_w = keep.tile([P, CHUNKS], F32, name="edge_w")

        def turn_weights(after):
            w_bank = take_bank(("weights",), after, [P, P])
            nc.tensor.transpose(w_bank[:], w_rows[:], ident[:])
            nc.scalar.copy(edge_w[:], w_bank[:, 0:CHUNKS])

        warm = keep.tile([P, 1], F32, name="warm")
        nc.scalar.activation(warm[:], ident[:, 0:1], SIGMOID)

        picked_plane = keep.tile([P, 2, J], U8, name="picked_plane", align_bytes=64)
        for side in (SRC, TGT):
            nc.vector.tensor_copy(picked_plane[:, side, :], tab_plane[:].indirect(lists[side][:]))

        picked_words = []

        def gather_words(h, tag):
            words = keep.tile([P, 2, HALF], U32, name="words%d" % h, tag=tag, align_bytes=64)
            for side in (SRC, TGT):
                window = tab_codes[:].bitcast(U32)
                nc.vector.tensor_copy(words[:, side, :], window.indirect(entries(lists[side], h * HALF, HALF)))
            picked_words.append(words)

        gather_words(0, "words0")

        wb_codes = keep.tile([P, N], U32, name="wb_codes", align_bytes=64)
        wb_plane = keep.tile([P, N], U8, name="wb_plane", align_bytes=64)
        for u, (part, cols) in enumerate(zip(wb_raw, wb_cols)):
            wb_bf = keep.tile([P, N // 2, PACK], BF16, name="wb_bf%d" % u, tag="wb_bf%d" % u, align_bytes=64)
            nc.scalar.copy(
                wb_bf[:].rearrange("p (c e) i -> p c i e", e=4),
                part[:].rearrange("p i (c e) -> p c i e", e=4),
            )
            grouped = wb_bf[:].rearrange("p n i -> p (n i)")
            nc.vector.quantize_mx(wb_codes[:, cols].bitcast(FP8X4), wb_plane[:, cols], grouped)

        gather_words(1, "wb_raw1")

        two_chunks = [
            keep.tile([P, 2, PACK, P], F32, name="gated%d" % q, tag="gated_then_woven%d" % q, align_bytes=64)
            for q in range(CHUNKS // 2)
        ]
        gated = [two_chunks[c // 2][:, c % 2, :, :] for c in range(CHUNKS)]

        def gate(c, ms_after, za_after):
            h = c // PER_HALF
            edges = slice(c * P, (c + 1) * P)
            in_half = slice((c % PER_HALF) * P, (c % PER_HALF + 1) * P)
            src_op = dict(lhsT=picked_words[h][:, SRC, in_half].bitcast(FP8X4), lhsT_scale=picked_plane[:, SRC, edges])
            tgt_op = dict(lhsT=picked_words[h][:, TGT, in_half].bitcast(FP8X4), lhsT_scale=picked_plane[:, TGT, edges])
            wa_op = dict(rhs=wa_codes[:].bitcast(FP8X4), rhs_scale=w_planes[:, WA, :])
            wb_op = dict(rhs=wb_codes[:].bitcast(FP8X4), rhs_scale=wb_plane[:])
            wc_op = dict(rhs=wc_codes[:].bitcast(FP8X4), rhs_scale=w_planes[:, WC, :])
            ms = take_bank(("ms", c), ms_after, [P, N])
            za = take_bank(("za", c), za_after, [P, N])
            nc.tensor.matmul_mx(ms[:], start=True, stop=True, **src_op, **wc_op)
            nc.tensor.matmul_mx(za[:], start=True, stop=False, **tgt_op, **wa_op)
            nc.tensor.matmul_mx(za[:], start=False, stop=True, **src_op, **wb_op)
            if c == CHUNKS - 1:
                eta = keep.tile([P, PACK, P], F32, name="last_eta")
                msg = keep.tile([P, PACK, P], F32, name="last_msg", tag="page3", align_bytes=64)
            elif c == CHUNKS - LATE_CHUNKS:
                eta = placed.tile([P, PACK, P], F32, name="held_eta", offset=HELD + 1024)
                msg = ring.tile([P, PACK, P], F32, name="msg")
            else:
                eta = ring.tile([P, PACK, P], F32, name="eta")
                msg = ring.tile([P, PACK, P], F32, name="msg")
            nc.scalar.activation(eta[:], za[:].rearrange("j (m i) -> j i m", i=PACK), SIGMOID)
            nc.scalar.activation(msg[:], ms[:].rearrange("j (m i) -> j i m", i=PACK), COPY, scale=edge_w[:, c : c + 1])
            nc.gpsimd.tensor_tensor(gated[c], msg[:], eta[:], MULT)

        turn_weights(None)
        for c in range(CHUNKS_IN_PSUM):
            gate(c, None, None)

        picked = {}

        def gather_r(i, first, count, rows):
            nc.vector.tensor_copy(rows[:], r_all[i][:].indirect(entries(tgt, first, count)))
            for b in range(count // P):
                picked[i, first // P + b] = rows[:, b * P : (b + 1) * P]

        gather_r(0, 0, J, keep.tile([P, J], F32, name="picked0"))
        gather_r(1, 0, J - QUARTER, keep.tile([P, J - QUARTER], F32, name="picked1"))
        gather_r(2, 0, P, placed.tile([P, P], F32, name="picked2_first", offset=HELD + 768))
        gather_r(2, P, J - P, keep.tile([P, J - P], F32, name="picked2_rest"))

        quarters = [(0, 0), (1, 0), (0, 1), (1, 1), (0, 2), (2, 0), (0, 3), (1, 2), (2, 1), (1, 3)]
        runs = [(i, q * QUARTER, QUARTER) for i, q in quarters]
        runs += [(2, J - QUARTER, QUARTER), (3, 0, HALF), (3, HALF, HALF - P), (3, J - P, P), (2, HALF, QUARTER)]
        pieces = [(1, CHUNKS - 2), (1, CHUNKS - 1)] + [(PACK - 1, c) for c in range(CHUNKS)]
        turns = dict(enumerate(runs))
        turns[5] = (EARLY_PAGES, P, P)
        turns["ahead"] = (EARLY_PAGES, 0, P)
        r_by_edge = {}

        turned_banks = {}

        def turn_r(k, after):
            i, first, count = turns[k]
            bank = take_bank(("turned", k), after, [P, count // P, P])
            for b in range(count // P):
                nc.tensor.transpose(bank[:, b, :], picked[i, first // P + b], ident[:])
            turned_banks[k] = bank

        def weigh_r(k):
            i, first, count = turns[k]
            bank = turned_banks[k]
            blocks = runs[k][2] // P if k in PLACES else 1
            turned = placed.tile([P, blocks, P], F32, name="r_by_edge%s" % k, offset=PLACES.get(k, AHEAD))
            for b in range(count // P):
                c = first // P + b
                nc.scalar.activation(turned[:, b, :], bank[:, b, :], COPY, scale=edge_w[:, c : c + 1])
                r_by_edge[i, c] = turned[:, b, :]

        last_sums = keep.tile([P, J], F32, name="last_sums")
        half_sums = keep.tile([P, HALF], F32, name="half_sums")
        sums = {}

        def add_and_turn_back(k, after):
            i, first, count = runs[k]
            bank = take_bank(("summed", k), after, [P, count // P, P])
            for b in range(count // P):
                terms = (r_by_edge[i, first // P + b], gated[first // P + b][:, i, :])
                for term, opens in zip(terms, (True, False)):
                    nc.tensor.matmul(bank[:, b, :], term, ident[:], start=opens, stop=not opens, is_transpose=True)
            if k == 0:
                sums[k] = placed.tile([P, count], F32, name="first_sums", offset=HELD)[:]
            elif i == EARLY_PAGES and first >= HALF:
                sums[k] = half_sums[:, first - HALF : first - HALF + count]
            elif i < PACK - 1:
                sums[k] = keep.tile([P, count], F32, name="sums_of_run%d" % k)[:]
            else:
                sums[k] = last_sums[:, first : first + count]
            nc.scalar.copy(sums[k], bank[:].rearrange("p b j -> p (b j)"))

        def scatter(i, first, values):
            nc.vector.tensor_copy(pages[i][:].indirect(entries(tgt, first, values.shape[1])), values)

        def step(k, before, piece):
            add_and_turn_back(k, before)
            if piece is not None:
                i, c = pieces[piece]
                gather_r(i, c * P, P, placed.tile([P, P], F32, name="piece%d" % k, offset=PLACES[k]))
            if k < len(quarters):
                scatter(runs[k][0], runs[k][1], sums[k])

        def turn_and_weigh(k, after):
            turn_r(k, after)
            weigh_r(k)

        turn_and_weigh(0, ("weights",))
        gate(3, ("ms", 0), ("za", 0))
        turn_r("ahead", ("turned", 0))
        step(0, None, None)
        turn_and_weigh(1, ("ms", 3))
        weigh_r("ahead")
        step(1, ("turned", "ahead"), 0)
        gate(4, ("ms", 1), ("za", 1))
        turn_and_weigh(2, ("za", 3))
        step(2, ("summed", 0), 1)
        gate(5, ("summed", 1), ("za", 2))
        turn_and_weigh(3, ("za", 5))
        step(3, ("za", 4), 2)
        gate(6, ("summed", 2), ("ms", 5))
        turn_and_weigh(4, ("turned", 2))
        gate(7, ("turned", 4), ("za", 6))
        clear_page(nc.gpsimd, "page3")
        turn_and_weigh(5, ("turned", 3))
        step(4, ("ms", 6), 3)
        turn_and_weigh(6, ("ms", 4))
        step(5, ("summed", 4), 4)
        turn_and_weigh(7, ("turned", 5))
        step(6, ("summed", 3), 5)
        turn_and_weigh(8, ("ms", 7))
        step(7, ("summed", 6), 6)
        turn_and_weigh(9, ("za", 7))
        step(8, ("summed", 7), 7)
        turn_and_weigh(14, ("summed", 5))
        step(14, ("turned", 14), None)
        turn_and_weigh(10, ("turned", 8))
        step(9, ("summed", 8), 8)
        turn_and_weigh(11, ("turned", 9))
        step(10, ("summed", 9), 9)
        scatter(EARLY_PAGES, HALF, half_sums[:])
        step(11, ("ms", 2), None)
        turn_and_weigh(12, ("turned", 11))
        step(12, ("turned", 10), None)
        turn_and_weigh(13, ("turned", 12))
        step(13, ("summed", 10), None)

        out_rows = out_0.rearrange("(p i) t -> p i t", i=PACK)
        shares = [(first, min(PIECE, GPSIMD_COLUMNS - first)) for first in range(0, GPSIMD_COLUMNS, PIECE)]
        woven = [
            keep.tile([P, width, PACK], BF16, name="woven%d" % q, align_bytes=64) for q, (first, width) in enumerate(shares)
        ]
        shares.append((GPSIMD_COLUMNS, T - GPSIMD_COLUMNS))
        last_tag = "gated_then_woven%d" % (CHUNKS // 2 - 1)
        woven.append(keep.tile([P, T - GPSIMD_COLUMNS, PACK], BF16, name="woven_last", tag=last_tag, align_bytes=64))

        def woven_columns(first, end):
            q = max(n for n, (start, width) in enumerate(shares) if start <= first)
            return woven[q][:, first - shares[q][0] : end - shares[q][0], :]

        for i in range(PACK):
            if i == PACK - 1:
                scatter(i, 0, last_sums[:])
            nc.sync.dma_start(out_rows[:, i, :], pages[i][:])
            if i == PACK - 1:
                break
            for q, (first, width) in enumerate(shares):
                piece = pages[i][:, first : first + width]
                if first >= GPSIMD_COLUMNS:
                    nc.scalar.copy(woven[q][:, :, i], piece)
                elif i == PACK - 2:
                    twice = piece.unsqueeze(2).to_broadcast([P, width, 2])
                    nc.gpsimd.tensor_scalar(woven[q][:, :, i:], twice, 1.0, 0.0, MULT, ADD)
                else:
                    nc.gpsimd.tensor_scalar(woven[q][:, :, i], piece, 1.0, 0.0, MULT, ADD)

        out_plane = keep.tile([P, PIECE], U8, name="out_plane", align_bytes=64)
        out_codes = keep.tile([P, T], I32, name="out_codes", align_bytes=64)
        out_words = words_of(out_1)
        spans = [(sum(SPAN_WIDTHS[:s]), width) for s, width in enumerate(SPAN_WIDTHS)]
        cuts = sorted(set([first for first, width in spans] + [VECTOR_COLUMNS, T]))
        copies = list(zip(cuts, cuts[1:]))

        def round_last(first, end):
            dst = woven_columns(first, end)[:, :, PACK - 1]
            if first < VECTOR_COLUMNS:
                nc.vector.tensor_copy(dst, pages[PACK - 1][:, first:end])
            else:
                nc.scalar.copy(dst, pages[PACK - 1][:, first:end])

        stored = 0
        rounded = 0
        for first, width in spans:
            ahead = [n for n, (start, end) in enumerate(copies) if start < first + width][-1] + 2
            for start, end in copies[rounded:ahead]:
                round_last(start, end)
            rounded = max(rounded, ahead)
            q, inner = divmod(first, PIECE)
            cols = slice(first, first + width)
            span = woven_columns(first, first + width).rearrange("p c i -> p (c i)")
            nc.vector.quantize_mx(out_codes[:, cols].bitcast(FP8X4), out_plane[4 * q :, inner : inner + width], span)
            if cols.stop in STORE_ENDS:
                nc.sync.dma_start(out_words[:, stored : cols.stop], out_codes[:, stored : cols.stop])
                stored = cols.stop
        for quad in range(QUADRANTS):
            queue = nc.sync if quad % 2 == 0 else nc.scalar
            rows = out_2[0, 4 * quad : 4 * quad + 4, :].bitcast(I32).rearrange("r (q c) -> q r c", q=PIECES)
            queue.dma_start(rows, out_plane[32 * quad : 32 * quad + 16, :].bitcast(I32))
